import numpy as np, ml_dtypes
CORES = [6,15,38,47]
N = 4
BF = ml_dtypes.bfloat16
P, L, B, T = 4096, 256, 1, 4
def skew(rng, n, hot):
    u = rng.random((N, 8, n))
    return np.take_along_axis(hot, np.minimum((P * u * u).astype(np.int64), P - 1), 2)
def parts(rng):
    x = rng.integers(0, 256, (N, 8, 16, P)); h = rng.integers(0, 256, (N, 8, 16, L))
    hot = np.argsort(rng.random((N, 8, P)), axis=2)
    pl = skew(rng, 16 * P, np.roll(hot, -1, axis=0)).reshape(N, 8, 16, P); kt = skew(rng, 16 * L, hot).reshape(N, 8, 16, L)
    nx = np.argsort(rng.random((N, 8, P)), axis=2); nx[:, 1::2] = skew(rng, P, hot)[:, 1::2]
    bm = rng.integers(0, P, (N, 8, L))
    th = np.stack([rng.integers(750, 1001, (N, 8)), rng.integers(900, 1251, (N, 8))], axis=2)
    return x, pl, nx, kt, h, bm, th
def pack(x, pl, nx, kt, h, bm, th):
    return {"xp": np.ascontiguousarray(x.reshape(N, 128, P)).astype(np.float32).astype(BF), "pl": np.ascontiguousarray(pl.reshape(N, 128, P)).astype(np.int32), "nx": np.ascontiguousarray(nx).astype(np.int32),
            "kt": np.ascontiguousarray(kt.reshape(N, 128, L)).astype(np.int32), "hm": np.ascontiguousarray(h.reshape(N, 128, L)).astype(np.float32).astype(BF), "bm": np.ascontiguousarray(bm).astype(np.int32), "th": np.ascontiguousarray(th).astype(np.int32)}
def setup_inputs(rng):
    return pack(*parts(rng))
def setup_inputs_spread(rng):
    x, pl, nx, kt, h, bm, th = parts(rng)
    x = np.minimum((rng.random(x.shape) * np.exp2(8.1 * rng.random((N, 8, 1, P)))).astype(np.int64), 255)
    h = np.minimum((rng.random(h.shape) * np.exp2(8.1 * rng.random((N, 8, 1, L)))).astype(np.int64), 255)
    th = np.minimum(np.exp2(12.0 * rng.random((N, 8, 2))).astype(np.int64), 4095); th[:, 2, 0] = rng.integers(300, 1200, N)
    hot = np.argsort(rng.random((N, 8, P)), axis=2); u = rng.random((N, 8, 16 * P)) ** 4
    pl = np.take_along_axis(np.roll(hot, -1, axis=0), np.minimum((P * u).astype(np.int64), P - 1), 2).reshape(N, 8, 16, P)
    nx[:, ::3] = skew(rng, P, hot)[:, ::3]
    return pack(x, pl, nx, kt, h, bm, th)
def edge(rng, n):
    return np.where(rng.random((N, 8, n)) < 0.7, (P - 1) * rng.integers(0, 2, (N, 8, n)), rng.integers(0, P, (N, 8, n)))
def setup_inputs_ends(rng):
    k = rng.integers(0, 5, (N, 8, 1, P)); x = np.where(k == 0, 0, np.where(k == 1, 255, 255 * rng.integers(0, 2, (N, 8, 16, P))))
    k = rng.integers(0, 8, (N, 8, 1, L)); h = np.where(k == 0, 0, np.where(k == 1, 255, np.where(k == 2, 127, 255 * rng.integers(0, 2, (N, 8, 16, L)))))
    x[..., 0] = 0; x[..., P - 1] = 255
    pl = edge(rng, 16 * P).reshape(N, 8, 16, P); kt = edge(rng, 16 * L).reshape(N, 8, 16, L); nx = edge(rng, P); bm = edge(rng, L)
    th = 4095 * np.ones((N, 8, 2), np.int64); th[:, :, 1] = 4095 * rng.integers(0, 2, (N, 8))
    for q in range(N):
        o = rng.permutation(7); th[q, o[:2], 0] = 0; th[q, o[2], 1] = 0; th[q, 7, 1] = 4095
        for g in range(8):
            if (q + g) % 4 == 0: nx[q, g, 0] = P - 1; nx[q, g, P - 1] = 0
            else: nx[q, g, 0] = rng.integers(7, P - 1); nx[q, g, P - 1] = rng.integers(7, P - 1)
        for g in (int(o[3]), 7):
            a = x[q, g]; a[:, [P - 1, 1, 2, 3]] = 255; a[:, [0, 4, 5, 6]] = 0
            kt[q, g, :, L - 1] = np.tile(np.array([P - 1, 1, 2, 3]), 4); h[q, g, :, L - 1] = 0
            kt[q, g, :, L - 2] = np.tile(np.array([5, 0, 4, 6]), 4); h[q, g, :, L - 2] = 255
    return pack(x, pl, nx, kt, h, bm, th)
def setup_inputs_corners(rng):
    x, pl, nx, kt, h, bm, th = parts(rng); pp = np.arange(P); kk = np.arange(16)[:, None]; li = np.arange(L)[None, :]
    for q in range(N):
        for g in range(8):
            b = (q - 1) % N; w = (g + q) % 8
            if w == 0: nx[q, g] = pp; th[q, g] = (4095, 4095)
            elif w == 1: nx[q, g] = pp ^ 1; th[q, g] = (1200, 0)
            elif w == 2:
                nx[q, g] = (pp + 1) % P; kt[q, g] = (P - 40 + li + kk) % P; pl[b, g] = (pp[None, :] + kk) % P; th[q, g] = (4095, 4095)
            elif w == 3:
                nx[q, g] = P - 1; bm[q, g] = np.where(li[0] % 3 == 0, 0, np.where(li[0] % 3 == 1, P - 1, li[0])); th[q, g] = (2000, 4095)
            elif w == 4:
                z = (0, P - 1, P // 2)[q % 3]; kt[q, g] = z; pl[b, g] = z; th[q, g] = (4095, 1100)
            elif w == 5:
                x[q, g] = x[q, g][:, pp - (pp & 7)]; th[q, g] = (2000, 1000)
                kt[q, g] = 8 * rng.integers(0, P // 8, (1, L)) + rng.integers(0, 8, (16, L)); pl[b, g] = 8 * rng.integers(0, P // 8, (1, P)) + rng.integers(0, 8, (16, P))
            elif w == 6:
                th[q, g] = (0, 4095); bm[q, g, 0] = 0; bm[q, g, L - 1] = P - 1; nx[q, g, 0] = 0
            else:
                kt[q, g] = (li + kk) & 15; pl[b, g] = rng.integers(0, 16, (16, P)); nx[q, g, :16] = (np.arange(16) + 1) & 15; th[q, g] = (4095, 4095)
    x[:, 7] = 255; h[:, 7] = 255; nx[:, 7] = pp; th[:, 7] = 4095
    kt[:, 7] = np.where(li < 31, 16 + li, (li + kk) & 15); pl[:, 7] = kk; pl[:, 7, :, 16:47] = 64 + np.arange(31)
    for q in range(N):
        b = (q - 1) % N; assert np.sum(np.any(~np.isin(pl[b, 7][:, kt[b, 7, 0]], kt[q, 7, 0]), axis=0)) == 31
    return pack(x, pl, nx, kt, h, bm, th)
def setup_inputs_ties(rng):
    x, pl, nx, kt, h, bm, th = parts(rng); t = rng.integers(40, 101, (N, 8, 1))
    far = t + np.where(rng.random((N, 8, P)) < 0.5, rng.integers(-1, 2, (N, 8, P)), rng.integers(0, 34, (N, 8, P)))
    x = 100 + np.where(np.arange(16)[:, None] == rng.integers(0, 16, (N, 8, 1, P)), far[:, :, None, :], 0)
    h = 100 + np.zeros((N, 8, 16, L), np.int64); h[:, :, 0] += (rng.random((N, 8, L)) < 0.125).astype(np.int64)
    order = np.argsort(far + rng.random(far.shape), axis=2); q = np.array([0.0, 0.2, 0.35, 0.55, 0.7, 0.9])
    def near(n, o):
        a = (P * rng.choice(q, (N, 8, 1, n))).astype(np.int64); i = np.minimum(a + ((P - a) * rng.random((N, 8, 16, n))).astype(np.int64), P - 1)
        return np.take_along_axis(o, i.reshape(N, 8, 16 * n), 2).reshape(N, 8, 16, n)
    kt = near(L, order); pl = near(P, np.roll(order, -1, axis=0))
    th = np.concatenate([t, ((t - 1) >> 1) + t + rng.integers(-1, 2, (N, 8, 1))], axis=2)
    return pack(x, pl, nx, kt, h, bm, th)
def sums(d):
    return (d[None, :] + ((np.arange(16)[:, None] + np.arange(d.shape[0])[None, :]) & 15)) >> 4
def setup_inputs_counts(rng):
    x, pl, nx, kt, h, bm, th = parts(rng); li = np.arange(L); kk = np.arange(16)[:, None]; gs = [int(g) for g in rng.permutation(8)]
    o = np.argsort(rng.random((N, 8, P)), axis=2)[:, :, :5 * L].reshape(N, 8, 5, L)
    h[:, gs[:6]] = 0
    for w in range(5):
        g = gs[w]; r = rng.permutation(L)
        for q in range(N):
            a, b, c, e, f = o[q, g]; a2, b2, c2, e2, f2 = o[(q + 1) % N, g]; pq = pl[q, g]; nq = nx[q, g]; kq = kt[q, g]
            if w < 2: t = 16 * int(rng.integers(128, 250)) + int(rng.choice(np.array([3, 4, 5, 11, 12, 13])))
            else: t = int(rng.integers(64, 4001))
            d = t + 40 + rng.integers(0, 41, P)
            if w == 0:
                d = t - 17 + rng.integers(0, 35, P); d[a] = t - 17 + li % 35; kq[:] = a; th[q, g, 0] = t
            elif w == 1:
                d = rng.integers(0, 4081, P); d[a] = 0; d[b] = t - 17 + li % 35; nq[a] = b; kq[:] = a; th[q, g] = (int(rng.integers(64, 4001)), t)
            elif w == 2:
                d[a] = 0; d[b] = t - 2 + li % 36; nq[a] = f; pq[:, a] = b2; kq[:] = a; th[q, g] = (t, 0)
            elif w == 3:
                m = r[:40]; v = r[40:53]
                d[a] = 0; d[b] = 0; d[c[m]] = t - 2 + np.arange(40) % 36
                nq[a] = f; nq[b] = f; nq[a[v]] = a[v]
                pq[:, a] = f2; pq[:, a[m]] = b2[m]; pq[:, a[v]] = a2[v][(np.arange(13) + kk) % 13]; pq[:, b[m]] = c2[m]
                kq[:] = a; th[q, g] = (t, 0)
            else:
                m = r[:52]; z = r[52:]
                d[a[m]] = 0; d[e[z]] = t - 2 + np.arange(L - 52) % 36
                nq[a[m[:-1]]] = a[m[1:]]; nq[a[m[-1]]] = f[0]; nq[b] = c; bm[q, g] = b
                pq[:, a] = f2; pq[:, b] = f2; pq[:, f] = f2; pq[:, c] = e2
                kq[:] = f; kq[:, m] = a[m]; th[q, g] = (t, 0)
            x[q, g] = sums(d)
    g = gs[5]; x[:, g] = 0; nx[:, g] = np.arange(P); th[:, g] = 4095
    kt[:, g] = np.where(li[None, :] < 31, 16 + li[None, :], (li[None, :] + kk) & 15); pl[:, g] = kk; pl[:, g, :, 16:47] = 64 + np.arange(31)
    return pack(x, pl, nx, kt, h, bm, th)
def check_inputs(d):
    bad = []
    for k, hi in (("xp", 255), ("pl", P - 1), ("nx", P - 1), ("kt", P - 1), ("hm", 255), ("bm", P - 1), ("th", 4095)):
        v = np.asarray(d[k]).astype(np.float64)
        if not (np.min(v) >= 0 and np.max(v) <= hi): bad.append("range of " + k)
        if k in ("xp", "hm") and np.any(v != np.floor(v)): bad.append("whole numbers of " + k)
    return bad
def pick(a, ix):
    return np.take_along_axis(a, ix[:, :, None, :], 3)
def mark(flags, y, go):
    a, g, i = np.nonzero(go); flags[a, g, y[a, g, i]] = True
def reference(xp, pl, nx, kt, hm, bm, th):
    x = xp.astype(np.float32).astype(np.int64).reshape(N, 8, 16, P); par = pl.astype(np.int64).reshape(N, 8, 16, P); nxt = nx.astype(np.int64)
    k = kt.astype(np.int64).reshape(N, 8, 16, L); h = hm.astype(np.float32).astype(np.int64).reshape(N, 8, 16, L)
    b = bm.astype(np.int64); t1 = th.astype(np.int64)[:, :, 0:1]; t2 = th.astype(np.int64)[:, :, 1:2]
    j = np.tile(np.arange(P, dtype=np.int64), (N, 8, 1)); eaten = np.zeros((N, 8, P), bool); a = np.zeros((N, 8, 1), np.int64)
    for t in range(T):
        c = np.take_along_axis(j, k.reshape(N, 8, 16 * L), 2).reshape(N, 8, 16, L)
        void = np.take_along_axis(eaten, c.reshape(N, 8, 16 * L), 2).reshape(N, 8, 16, L)
        d = np.stack([np.add.reduce(np.abs(pick(x, c[:, :, i]) - h), axis=2) for i in range(16)], axis=2)
        d = np.where(void, 2 ** 20, d)
        w = np.argmin(d, axis=2)[:, :, None, :]
        hit = np.take_along_axis(d, w, 2)[:, :, 0] < t1 + (a & 31)
        y = np.where(hit, np.take_along_axis(c, w, 2)[:, :, 0], np.take_along_axis(j, b, 2))
        new = np.zeros((N, 8, P), bool); go = hit
        h = np.where(go[:, :, None, :], (h + pick(x, y)) >> 1, h); mark(new, y, go)
        for s in range(B):
            n = np.take_along_axis(j, np.take_along_axis(nxt, y, 2), 2); xn = pick(x, n)
            go = go & ~np.take_along_axis(eaten, n, 2) & (np.add.reduce(np.abs(xn - h), axis=2) <= t2)
            y = np.where(go, n, y); h = np.where(go[:, :, None, :], (h + xn) >> 1, h); mark(new, y, go)
        b = np.take_along_axis(nxt, y, 2); a = np.add.reduce(hit.astype(np.int64), axis=2, keepdims=True)
        j = np.where(new, nxt, j); eaten = eaten | new
        j = np.take_along_axis(j, j, 2)
        if t < T - 1:
            k = np.roll(pick(par, y), 1, axis=0); h = np.roll(h, 1, axis=0)
    return {"yj": j.astype(np.float32), "yh": h.reshape(N, 128, L).astype(np.float32).astype(BF), "yb": b.astype(np.float32)}

@@ -1,0 +1,507 @@
+from concourse.bass import DstId, RemoteDMATransfer
+from concourse.mybir import dt, AluOpType, AxisListType, ActivationFunctionType
+
+A_ = AluOpType
+F = ActivationFunctionType
+CHUNKS = [(0, 96), (96, 192), (192, 256)]
+BIAS = 262144.0
+NV = 4
+NSLOT = 8
+
+
+def _sb(n, d="float32", p=128):
+    return ("sbuf", [p, n], d)
+
+
+SCRATCH = {
+    "BIG": _sb(8448), "X": _sb(4096, "bfloat16"), "NX": _sb(4096, "int32"), "PL": _sb(4096, "int32"),
+    "JH": _sb(4096, "float16"), "JR": _sb(4096), "Q": _sb(4096),
+    "S": ("sbuf", [128, 256, 16], "float16"), "RL": ("sbuf", [128, 256, 16], "float16"),
+    "ER2": _sb(2048, "float16"), "ERM": _sb(2048, "float16"), "EX": _sb(2048, "float16"), "BR": _sb(2048, "float16"),
+    "IB": _sb(128, "bfloat16"), "IH": _sb(128, "float16"), "BO": _sb(128), "BO8": _sb(8, "float16"),
+    "APA": _sb(128, "bfloat16"), "IOB": _sb(256, "bfloat16"), "OH": _sb(16), "DM": _sb(256), "RS": _sb(256), "RM": _sb(256),
+    "KC": _sb(256, "float16"), "CM": _sb(256, "float16"), "ZN": _sb(512, "float16"), "ZS": _sb(512, "float16"),
+    "ZW": _sb(128, "float16"), "LB": _sb(128), "T0": _sb(512), "T1": _sb(512), "PI": _sb(2, "int32"),
+    "PJ": _sb(2, "int32"), "FC": _sb(2), "GC": _sb(2), "FS": _sb(2), "PC": _sb(2),
+    "KI": _sb(256, "int32"), "HB": _sb(256, "bfloat16"), "THI": _sb(2, "int32"), "THF": _sb(2), "BMI": _sb(256, "int32"),
+    "BMF": _sb(256), "TT": _sb(2), "THR": _sb(2), "TB": _sb(2),
+    "K0": _sb(256, "uint16"), "K1": _sb(256, "uint16"), "K2": _sb(256, "uint16"), "K3": _sb(256, "uint16"),
+    "H0": _sb(256, "float16"), "H1": _sb(256, "float16"), "H2": _sb(256, "float16"), "H3": _sb(256, "float16"),
+    "KS0": _sb(256, "uint16"), "KS1": _sb(256, "uint16"), "KS2": _sb(256, "uint16"),
+    "HS0": _sb(256, "float16"), "HS1": _sb(256, "float16"), "HS2": _sb(256, "float16"), "HS3": _sb(256, "float16"),
+    "HA": _sb(256, "float16"),
+    "PS": _sb(256), "SC": _sb(256), "Z": _sb(256), "F1": _sb(256), "SS": _sb(256), "S2": _sb(256, "float16"), "R2": _sb(256, "float16"),
+    "MT": _sb(16), "MKI": _sb(16, "int32"), "KWI": _sb(16, "int32"), "LI": _sb(16), "E1": _sb(16), "E2": _sb(16), "HI": _sb(16), "B16": _sb(16),
+    "U1": _sb(16), "U2": _sb(16), "QF": _sb(16), "QXF": _sb(16), "QO": _sb(16, "uint16"), "QXO": _sb(16, "uint16"),
+    "VI": _sb(16, "int32"), "FR": _sb(16), "YL": _sb(16), "YO": _sb(16, "uint16"), "VL": _sb(16), "VO": _sb(16, "uint16"), "NL": _sb(16),
+    "GO": _sb(16), "W1": _sb(16), "W2": _sb(16), "YF": _sb(16), "YFO": _sb(16, "uint16"), "QNF": _sb(16), "QNO": _sb(16, "uint16"),
+    "WI": _sb(16, "int32"), "AB": _sb(32, "int32"), "ABY": _sb(32), "ABN": _sb(32), "Y16": _sb(16),
+    "LA": _sb(128 * NSLOT, "bfloat16"), "RB": _sb(256 * NSLOT, "bfloat16"),
+    "CNT": _sb(2), "MSK": _sb(256), "C16": _sb(256, "float16"), "DX": _sb(256), "JC": _sb(256), "J16": _sb(256, "float16"),
+    "LP": _sb(256, "uint16"), "I1": _sb(256, "int32"), "I2": _sb(256, "int32"), "I3": _sb(256, "int32"), "PSG": _sb(256),
+    "YB": _sb(256), "YH": _sb(256, "bfloat16"),
+    "R0": ("psum", [128, 512], "float32"), "R1": ("psum", [128, 512], "float32"),
+    "R2P": ("psum", [128, 512], "float32"), "R3": ("psum", [128, 512], "float32"),
+    "KEY": ("psum", [128, 512], "float32"), "HP": ("psum", [128, 512], "float32"),
+    "CN": ("psum", [128, 512], "float32"), "SM": ("psum", [128, 512], "float32"),
+}
+RING = ["R0", "R1", "R2P", "R3"]
+PSUM = RING + ["KEY", "HP", "CN", "SM"]
+NDMA = 60
+SEMAPHORES = ["cV", "cA", "cT", "cG"] + ["d%d" % i for i in range(NDMA)] + ["rh%d" % t for t in range(3)] + ["rk%d" % t for t in range(3)] + ["ls"]
+
+
+def rank_program(g, core, T, topo):
+    rank = T.rank_of(core)
+    if rank is None:
+        return
+    queue = {"V": g.vector, "A": g.scalar, "T": g.tensor, "G": g, "S": g.sync}
+    count = {"V": 0, "A": 0, "T": 0, "G": 0}
+    known = {"V": {}, "A": {}, "T": {}, "G": {}, "S": {}}
+    snap = {}
+    acc = {}
+    ndma = [0]
+
+    def need(q, sem, val):
+        k = known[q]
+        if k.get(sem, 0) >= val:
+            return
+        queue[q].wait_ge(T.sem[sem], val)
+        k[sem] = val
+        for s, v in snap.get((sem, val), {}).items():
+            if k.get(s, 0) < v:
+                k[s] = v
+
+    def span(a):
+        return a if len(a) == 3 else (a[0], 0, 1 << 30)
+
+    def deps(q, reads, writes, group):
+        w = {}
+        for lst, wr in ((reads, False), (writes, True)):
+            for a in lst:
+                b, lo, hi = span(a)
+                for (l, h, ow, oq, s, v, gr) in acc.get(b, []):
+                    if b in PSUM and oq != q:
+                        pass
+                    elif not (lo < h and l < hi) or not (wr or ow):
+                        continue
+                    elif group is not None and gr == group:
+                        continue
+                    if w.get(s, 0) < v:
+                        w[s] = v
+        for s, v in sorted(w.items(), key=lambda e: -len(snap.get(e, {}))):
+            need(q, s, v)
+
+    def note(q, reads, writes, sem, val, group):
+        snap[(sem, val)] = dict(known[q]) if q in known else {}
+        for lst, wr in ((reads, False), (writes, True)):
+            for a in lst:
+                b, lo, hi = span(a)
+                old = acc.get(b, [])
+                if wr:
+                    old = [e for e in old if not (lo <= e[0] and e[1] <= hi and known.get(q, {}).get(e[4], 0) >= e[5])]
+                else:
+                    old = [e for e in old if not (not e[2] and e[3] == q and lo <= e[0] and e[1] <= hi and e[4] == sem)]
+                old.append((lo, hi, wr, q, sem, val, group))
+                acc[b] = old
+
+    def op(q, fn, reads, writes, group=None):
+        deps(q, reads, writes, group)
+        count[q] += 1
+        fn().then_inc(T.sem["c" + q], 1)
+        note(q, reads, writes, "c" + q, count[q], group)
+
+    def dma(q, out, in_, reads, writes, ndep=1):
+        deps(q, reads, writes, None)
+        name = "d%d" % ndma[0]
+        ndma[0] += 1
+        queue[q].dma_start(out, in_).then_inc(T.sem[name], 16)
+        note("dma", reads, writes, name, 16, None)
+        snap[(name, 16)] = dict(known[q])
+        return name
+
+    def dmas(q, pairs, writes):
+        name = "d%d" % ndma[0]
+        ndma[0] += 1
+        for o, i in pairs:
+            queue[q].dma_start(o, i).then_inc(T.sem[name], 16)
+        note("dma", [], writes, name, 16 * len(pairs), None)
+
+    V, S_, TE = g.vector, g.scalar, g.tensor
+
+    def tcopy(out, in_, r, w):
+        op("V", lambda: V.tensor_copy(out, in_), r, w)
+
+    def tt(out, a, b, o, r, w):
+        op("V", lambda: V.tensor_tensor(out, a, b, o), r, w)
+
+    def ts(out, a, s1, s2, o0, o1, r, w):
+        if o1 is None:
+            op("V", lambda: V.tensor_scalar(out, a, s1, s2, o0), r, w)
+        else:
+            op("V", lambda: V.tensor_scalar(out, a, s1, s2, o0, o1), r, w)
+
+    def act(out, in_, r, w, bias=0.0, scale=1.0):
+        op("A", lambda: S_.activation(out, in_, F.Identity, bias=bias, scale=scale), r, w)
+
+    def scan(out, d0, d1, o0, o1, r, w):
+        op("V", lambda: V.tensor_tensor_scan(out, d0, d1, 0.0, o0, o1), r, w)
+
+    def mm(out, l, rh, st, sp, r, w, group):
+        op("T", lambda: TE.matmul(out, l, rh, st, sp), r, w, group)
+
+    def iota(out, pat, base, cm, w):
+        op("G", lambda: g.iota(out, pat, base, cm, allow_small_or_imprecise_dtypes=True), [], w)
+
+    gid = [0]
+
+    def newgroup():
+        gid[0] += 1
+        return gid[0]
+
+    dma("S", T.KI[:], T.kt[:], [], [("KI",)])
+    dma("S", T.HB[:], T.hm[:], [], [("HB",)])
+    for j in range(4):
+        dma("S", T.X[:, 1024 * j:1024 * j + 1024], T.xp[:, 1024 * j:1024 * j + 1024], [], [("X", 1024 * j, 1024 * j + 1024)])
+    dma("A", T.THI[0:8, :], T.th[:], [], [("THI",)])
+    dma("A", T.BMI[0:8, :], T.bm[:], [], [("BMI",)])
+    dmas("S", [(T.NX[k:128:16, :], T.nx[:]) for k in range(16)], [("NX",)])
+    dma("S", T.PL[:], T.pl[:], [], [("PL",)])
+
+    op("G", lambda: g.iota(T.PI[:], [[0, 2]], 0, 1), [], [("PI",)])
+    iota(T.T0[:, 0:128], [[1, 8], [0, 16]], 0, 0, [("T0", 0, 128)])
+    iota(T.T0[:, 128:256], [[0, 8], [1, 16]], 0, 0, [("T0", 128, 256)])
+    iota(T.T1[:, 0:256], [[0, 16], [1, 16]], 0, 0, [("T1", 0, 256)])
+    iota(T.T1[:, 256:512], [[1, 256]], 0, 0, [("T1", 256, 512)])
+    iota(T.T0[:, 256:384], [[1, 128]], 0, -1, [("T0", 256, 384)])
+    iota(T.T0[0:8, 384:512], [[1, 8], [0, 16]], 0, -1, [("T0", 384, 512)])
+    iota(T.B16[:], [[16, 16]], 0, 0, [("B16",)])
+    ts(T.PJ[:], T.PI[:], 15, None, A_.bitwise_and, None, [("PI",)], [("PJ",)])
+    tcopy(T.FC[:], T.PJ[:], [("PJ",)], [("FC",)])
+    ts(T.PI[:], T.PI[:], 4, None, A_.arith_shift_right, None, [("PI",)], [("PI",)])
+    tcopy(T.GC[:], T.PI[:], [("PI",)], [("GC",)])
+    ts(T.FS[:], T.FC[:], 256.0, None, A_.mult, None, [("FC",)], [("FS",)])
+    fcol, gcol = T.FC[:, 0:1], T.GC[:, 0:1]
+    tcopy(T.K0[:], T.KI[:], [("KI",)], [("K0",)])
+    ts(T.H0[:], T.HB[:], 1026.0, None, A_.add, None, [("HB",)], [("H0",)])
+    ts(T.IB[:], T.T0[:, 256:384], 0.0, None, A_.is_equal, None, [("T0", 256, 384)], [("IB",)])
+    ts(T.IH[:], T.T0[:, 256:384], 0.0, None, A_.is_equal, None, [("T0", 256, 384)], [("IH",)])
+    ts(T.ZW[:], T.T0[:, 256:384], 0.0, 1.0 / 8192, A_.is_equal, A_.mult, [("T0", 256, 384)], [("ZW",)])
+    ts(T.ZN[:, 0:256], T.T1[:, 256:512], -256.0, None, A_.add, None, [("T1", 256, 512)], [("ZN", 0, 256)])
+    tcopy(T.ZN[:, 256:512], T.T1[:, 256:512], [("T1", 256, 512)], [("ZN", 256, 512)])
+
+    def ring_evac(n, fill, evac):
+        for i in range(n):
+            fill(i, RING[i % 4])
+            evac(i, RING[i % 4])
+
+    def fill0(i, r):
+        gr = newgroup()
+        mm(T[r][:], T.IB[:], T.X[:, 512 * i:512 * i + 512], True, False, [("IB",), ("X", 512 * i, 512 * i + 512)], [(r,)], gr)
+        mm(T[r][:], T.ZW[:], T.ZN[:], False, True, [("ZW",), ("ZN",)], [(r,)], gr)
+
+    def evac0(i, r):
+        b = 1024.0 + (512 * i + 256 - 2048) / 8192.0
+        w = [("BIG", 512 * i, 512 * i + 512)]
+        if i % 2:
+            act(T.BIG[:, 512 * i:512 * i + 512], T[r][:], [(r,)], w, bias=b)
+        else:
+            ts(T.BIG[:, 512 * i:512 * i + 512], T[r][:], b, None, A_.add, None, [(r,)], w)
+
+    ring_evac(8, fill0, evac0)
+
+    op("V", lambda: V.tensor_scalar(T.CM[:], T.T1[:, 0:256], 0.0, -1026.0, A_.mult, A_.add), [("T1", 0, 256)], [("CM",)])
+    tcopy(T.KC[:], T.T1[:, 0:256], [("T1", 0, 256)], [("KC",)])
+    ts(T.BO8[:], T.T1[:, 256:264], gcol, 32.0, A_.is_equal, A_.mult, [("T1", 256, 512), ("GC",)], [("BO8",)])
+    for r in range(4):
+        ts(T.ER2[:, 512 * r:512 * r + 512], T.T1[:], 0.0, None, A_.mult, None, [("T1",)], [("ER2", 512 * r, 512 * r + 512)])
+    for r in range(16):
+        tcopy(T.ER2[:, 128 * r + r:128 * r + 128:16], T.BO8[:], [("BO8",), ("ER2", 128 * r, 128 * r + 128)], [("ER2", 128 * r, 128 * r + 128)])
+    ts(T.ERM[:], T.ER2[:], -0.5, None, A_.mult, None, [("ER2",)], [("ERM",)])
+    ts(T.OH[:], T.T1[:, 256:272], fcol, None, A_.is_equal, None, [("T1", 256, 512), ("FC",)], [("OH",)])
+    ts(T.DM[:], T.T1[:, 0:256], fcol, None, A_.is_equal, None, [("T1", 0, 256), ("FC",)], [("DM",)])
+    ts(T.RS[:], T.T1[:, 0:256], 0.0, None, A_.is_gt, None, [("T1", 0, 256)], [("RS",)])
+    ts(T.RM[:], T.RS[:], -2.0e9, 1.0e9, A_.mult, A_.add, [("RS",)], [("RM",)])
+    ts(T.BO[:], T.T0[:, 0:128], gcol, None, A_.is_equal, None, [("T0", 0, 128), ("GC",)], [("BO",)])
+    ts(T.LB[0:8, :], T.T0[0:8, 384:512], 0.0, None, A_.is_equal, None, [("T0", 384, 512)], [("LB",)])
+    ts(T.LI[:], T.B16[:], fcol, None, A_.add, None, [("B16",), ("FC",)], [("LI",)])
+    ts(T.HI[:], T.LI[:], 8192.0, None, A_.add, None, [("LI",)], [("HI",)])
+    ts(T.E2[:], T.LI[:], 15.0, -4096.0, A_.mult, A_.add, [("LI",)], [("E2",)])
+    tcopy(T.THF[0:8, :], T.THI[0:8, :], [("THI",)], [("THF",)])
+    tcopy(T.BMF[0:8, :], T.BMI[0:8, :], [("BMI",)], [("BMF",)])
+    mm(T.SM[:, 0:2], T.LB[0:8, :], T.THF[0:8, :], True, True, [("LB",), ("THF",)], [("SM", 0, 2)], newgroup())
+    mm(T.SM[:, 256:512], T.LB[0:8, :], T.BMF[0:8, :], True, True, [("LB",), ("BMF",)], [("SM", 256, 512)], newgroup())
+    ts(T.TT[:], T.SM[:, 0:2], 16.0, -BIAS, A_.mult, A_.add, [("SM", 0, 2)], [("TT",)])
+    tcopy(T.THR[:], T.TT[:], [("TT",)], [("THR",)])
+    tt(T.Z[:], T.SM[:, 256:512], T.DM[:], A_.mult, [("SM", 256, 512), ("DM",)], [("Z",)])
+    scan(T.SC[:], T.RS[:], T.Z[:], A_.mult, A_.add, [("RS",), ("Z",)], [("SC",)])
+    tcopy(T.B16[:], T.SC[:, 15:256:16], [("SC",)], [("B16",)])
+
+    def setup_late():
+        ts(T.APA[:], T.T0[:, 128:256], 1.0, None, A_.add, None, [("T0", 128, 256)], [("APA",)])
+        tt(T.APA[:], T.APA[:], T.BO[:], A_.mult, [("APA",), ("BO",)], [("APA",)])
+        ts(T.APA[:], T.APA[:], -1.0, None, A_.add, None, [("APA",)], [("APA",)])
+        ts(T.IOB[:], T.T1[:, 256:512], 1.0, None, A_.add, None, [("T1", 256, 512)], [("IOB",)])
+        for k in range(16):
+            c = (128 * k, 128 * k + 128)
+            ts(T.EX[:, c[0]:c[1]], T.IH[:], T.OH[:, k:k + 1], None, A_.mult, None, [("IH",), ("OH",)], [("EX",) + c])
+            ts(T.BR[:, c[0]:c[1]], T.BO[:], T.OH[:, k:k + 1], None, A_.mult, None, [("BO",), ("OH",)], [("BR",) + c])
+        ts(T.ZS[:, 0:256], T.T1[:, 256:512], 16.0, -2048.0, A_.mult, A_.add, [("T1", 256, 512)], [("ZS", 0, 256)])
+        ts(T.ZS[:, 256:512], T.T1[:, 256:512], 16.0, -2047.0, A_.mult, A_.add, [("T1", 256, 512)], [("ZS", 256, 512)])
+        ts(T.PSG[:], T.T1[:, 256:512], T.FS[:, 0:1], None, A_.add, None, [("T1", 256, 512), ("FS",)], [("PSG",)])
+        tcopy(T.JC[:], T.PSG[:], [("PSG",)], [("JC",)])
+        op("V", lambda: V.memset(T.MSK[:], 0.0), [], [("MSK",)])
+
+    def extract(lo, hi, first):
+        gr = newgroup()
+        for k in range(16):
+            mm(T.KEY[:, lo:hi], T.EX[:, 128 * k:128 * k + 128], T.JH[:, 16 * lo + k:16 * hi:16], k == 0, k == 15,
+               [("EX",), ("JH", 16 * lo, 16 * hi)], [("KEY", lo, hi)], gr)
+
+    def nx_tables():
+        for j in range(4):
+            c = (1024 * j, 1024 * j + 1024)
+            ts(T.JH[:, c[0]:c[1]], T.NX[:, c[0]:c[1]], -2048.0, None, A_.add, None, [("NX",) + c], [("JH",) + c])
+
+    def nx_tables2():
+        extract(0, 256, True)
+        ts(T.I1[:], T.KEY[:, 0:256], 2048.0, None, A_.add, None, [("KEY", 0, 256)], [("I1",)])
+        ts(T.I2[:], T.I1[:], 15, None, A_.bitwise_and, None, [("I1",)], [("I2",)])
+        ts(T.I3[:], T.I1[:], 4, None, A_.arith_shift_right, None, [("I1",)], [("I3",)])
+        ts(T.DX[:], T.I2[:], 256.0, None, A_.mult, None, [("I2",)], [("DX",)])
+        tt(T.DX[:], T.DX[:], T.I3[:], A_.add, [("DX",), ("I3",)], [("DX",)])
+        tt(T.DX[:], T.DX[:], T.PSG[:], A_.subtract, [("DX",), ("PSG",)], [("DX",)])
+
+    BW = ("BIG", 0, 8448)
+    nslot = [0]
+
+    def codes(src, gate, dst):
+        ts(T.Y16[:], T[src][:], 16.0, None, A_.add, None, [(src,)], [("Y16",)])
+        tt(T.WI[:], T.Y16[:], T[gate][:], A_.mult, [("Y16",), (gate,)], [("WI",)])
+        ts(T.AB[:, 0:16], T.WI[:], 15, None, A_.bitwise_and, None, [("WI",)], [("AB", 0, 16)])
+        ts(T.AB[:, 16:32], T.WI[:], 4, None, A_.arith_shift_right, None, [("WI",)], [("AB", 16, 32)])
+        tcopy(T[dst][:], T.AB[:], [("AB",)], [(dst,)])
+
+    def marks(src, cols, first, last, gr):
+        for c in cols:
+            s = nslot[0] % NSLOT
+            nslot[0] += 1
+            la, rb = ("LA", 128 * s, 128 * s + 128), ("RB", 256 * s, 256 * s + 256)
+            ts(T.LA[:, la[1]:la[2]], T.APA[:], T[src][:, c:c + 1], None, A_.is_equal, None, [("APA",), (src,)], [la])
+            ts(T.RB[:, rb[1]:rb[2]], T.IOB[:], T[src][:, 16 + c:17 + c], None, A_.is_equal, None, [("IOB",), (src,)], [rb])
+            mm(T.CN[:, 0:256], T.LA[:, la[1]:la[2]], T.RB[:, rb[1]:rb[2]], first and c == 0, last and c == 15, [la, rb], [("CN", 0, 256)], gr)
+
+    def to_hp(h):
+        gr = newgroup()
+        mm(T.HP[:, 0:256], T.IH[:], T[h][:], True, False, [("IH",), (h,)], [("HP", 0, 256)], gr)
+        mm(T.HP[:, 0:256], T.IH[:], T.CM[:], False, True, [("IH",), ("CM",)], [("HP", 0, 256)], gr)
+        act(T.BIG[:, 8192:8448], T.HP[:, 0:256], [("HP", 0, 256)], [("BIG", 8192, 8448)], bias=1024.0)
+
+    def pull(win, wr, off, dst):
+        tt(T.Z[:], win.indirect(T[off][:]), T.DM[:], A_.mult, [wr, (off,), ("DM",)], [("Z",)])
+        scan(T.SC[:], T.RS[:], T.Z[:], A_.mult, A_.add, [("RS",), ("Z",)], [("SC",)])
+
+    def place(dst):
+        tcopy(T.VI[:], T.SC[:, 15:256:16], [("SC",)], [("VI",)])
+        tt(T.FR[:], T.SC[:, 15:256:16], T.VI[:], A_.subtract, [("SC",), ("VI",)], [("FR",)])
+        ts(T[dst][:], T.FR[:], 8192.0, 2048.0, A_.mult, A_.add, [("FR",)], [(dst,)])
+
+    def blend(out):
+        tt(T.SS[:], T.F1[:], T.HP[:, 0:256], A_.add, [("F1",), ("HP", 0, 256)], [("SS",)])
+        ts(T[out][:], T.SS[:], 0.5, 513.75, A_.mult, A_.add, [("SS",)], [(out,)])
+
+    nxt = T.cores[(rank + 1) % len(T.cores)]
+    mask = topo.mask(core, nxt)
+    rid, pid, _s = topo.addr(nxt)
+    prv = T.cores[(rank - 1) % len(T.cores)]
+    neng = len(topo.engines(core, nxt))
+    nprv = len(topo.engines(prv, core))
+    sent = [0]
+
+    def send(dst, src, sem):
+        deps("G", [(src,)], [], None)
+        g.remote_dma(T[dst][:], T[src][:], T.sem[sem], T.sem.ls, pid, rid, mask)
+        sent[0] += neng
+
+    def arrive(dst, sem):
+        note("remote", [], [(dst,)], sem, nprv, None)
+
+    for t in range(NV):
+        last = t == NV - 1
+        kb, hb, hs = "K%d" % t, "H%d" % t, "HS%d" % t
+        to_hp(hb)
+        for (l0, l1) in CHUNKS:
+            xc = ("BIG", 4096 + 16 * l0, 4096 + 16 * l1)
+            act(T.BIG[:, xc[1]:xc[2]], T.BIG[:, 0:4096].indirect(T[kb][:, l0:l1]), [("BIG", 0, 4096), (kb,)], [xc])
+        if t == 0:
+            setup_late()
+            nx_tables()
+        tt(T.E1[:], T.HI[:], T.E2[:], A_.add, [("HI",), ("E2",)], [("E1",)])
+        tt(T.E1[:], T.E1[:], T.B16[:], A_.subtract, [("E1",), ("B16",)], [("E1",)])
+        kgr = newgroup()
+        for (l0, l1) in CHUNKS:
+            s3 = ("S", 16 * l0, 16 * l1)
+            r3 = ("RL", 16 * l0, 16 * l1)
+            ko = ("KEY", l0, l1)
+            for k in range(16):
+                a = 4096 + 16 * l0
+                op("V", lambda k=k, a=a: V.tensor_tensor(T.S[:, l0:l1, k], T.BIG[:, a + k:4096 + 16 * l1:16], T.HP[:, l0:l1], A_.subtract),
+                   [("BIG", a, 4096 + 16 * l1), ("HP", 0, 256)], [s3], "s%d_%d" % (t, l0))
+            ts(T.RL[:, l0:l1, :], T.S[:, l0:l1, :], -1024.0, 0.0, A_.add, A_.max, [s3], [r3])
+            mm(T.KEY[:, l0:l1], T.IH[:], T.KC[:, l0:l1], True, False, [("IH",), ("KC",)], [ko], kgr)
+            for r in range(16):
+                mm(T.KEY[:, l0:l1], T.ERM[:, 128 * r:128 * r + 128], T.S[:, l0 + r:l1:16, :], False, False, [("ERM",), s3], [ko], kgr)
+            for r in range(16):
+                mm(T.KEY[:, l0:l1], T.ER2[:, 128 * r:128 * r + 128], T.RL[:, l0 + r:l1:16, :], False, r == 15, [("ER2",), r3], [ko], kgr)
+        scan(T.PS[:], T.RM[:], T.KEY[:, 0:256], A_.max, A_.min, [("RM",), ("KEY", 0, 256)], [("PS",)])
+        mk = T.PS[:, 15:256:16]
+        tcopy(T.MKI[:], mk, [("PS",)], [("MKI",)])
+        ts(T.MT[:], mk, T.THR[:, 0:1], None, A_.is_lt, None, [("PS",), ("THR",)], [("MT",)])
+        ts(T.KWI[:], T.MKI[:], 15, None, A_.bitwise_and, None, [("MKI",)], [("KWI",)])
+        tt(T.U2[:], T.KWI[:], T.E2[:], A_.add, [("KWI",), ("E2",)], [("U2",)])
+        tt(T.U1[:], T.KWI[:], T.E1[:], A_.add, [("KWI",), ("E1",)], [("U1",)])
+        tt(T.U2[:], T.U2[:], T.MT[:], A_.mult, [("U2",), ("MT",)], [("U2",)])
+        tt(T.U1[:], T.U1[:], T.MT[:], A_.mult, [("U1",), ("MT",)], [("U1",)])
+        tt(T.QXF[:], T.U2[:], T.HI[:], A_.add, [("U2",), ("HI",)], [("QXF",)])
+        tt(T.QF[:], T.U1[:], T.B16[:], A_.add, [("U1",), ("B16",)], [("QF",)])
+        tcopy(T.QXO[:], T.QXF[:], [("QXF",)], [("QXO",)])
+        tcopy(T.QO[:], T.QF[:], [("QF",)], [("QO",)])
+        act(T.F1[:], T.BIG[:].indirect(T.QXO[:]), [BW, ("QXO",)], [("F1",)])
+        pull(T.BIG[:], BW, "QO", None)
+        place("YL")
+        tcopy(T.YO[:], T.YL[:], [("YL",)], [("YO",)])
+        pull(T.NX[:], ("NX",), "YO", None)
+        tcopy(T.VO[:], T.SC[:, 15:256:16], [("SC",)], [("VO",)])
+        tcopy(T.VL[:], T.SC[:, 15:256:16], [("SC",)], [("VL",)])
+        blend("HA")
+        act(T.F1[:], T.BIG[:, 0:4096].indirect(T.VO[:]), [("BIG", 0, 4096), ("VO",)], [("F1",)])
+        to_hp("HA")
+        pull(T.BIG[:, 0:4096], ("BIG", 0, 4096), "VO", None)
+        tt(T.S2[:], T.F1[:], T.HP[:, 0:256], A_.subtract, [("F1",), ("HP", 0, 256)], [("S2",)])
+        ts(T.R2[:], T.S2[:], -1024.0, 0.0, A_.add, A_.max, [("S2",)], [("R2",)])
+        g2 = newgroup()
+        for r in range(16):
+            mm(T.SM[:, 0:16], T.ERM[:, 128 * r:128 * r + 128], T.S2[:, r:256:16], r == 0, False, [("ERM",), ("S2",)], [("SM", 0, 16)], g2)
+        for r in range(16):
+            mm(T.SM[:, 0:16], T.ER2[:, 128 * r:128 * r + 128], T.R2[:, r:256:16], False, r == 15, [("ER2",), ("R2",)], [("SM", 0, 16)], g2)
+        place("NL")
+        tt(T.W1[:], T.VL[:], T.HI[:], A_.subtract, [("VL",), ("HI",)], [("W1",)])
+        tt(T.W2[:], T.NL[:], T.YL[:], A_.subtract, [("NL",), ("YL",)], [("W2",)])
+        codes("YL", "MT", "ABY")
+        gm = newgroup()
+        marks("ABY", range(0, 3), True, False, gm)
+        ts(T.GO[:], T.SM[:, 0:16], T.TT[:, 1:2], None, A_.is_le, None, [("SM", 0, 16), ("TT",)], [("GO",)])
+        tt(T.GO[:], T.GO[:], T.MT[:], A_.mult, [("GO",), ("MT",)], [("GO",)])
+        tt(T.W1[:], T.W1[:], T.GO[:], A_.mult, [("W1",), ("GO",)], [("W1",)])
+        tt(T.W2[:], T.W2[:], T.GO[:], A_.mult, [("W2",), ("GO",)], [("W2",)])
+        tt(T.QNF[:], T.W1[:], T.HI[:], A_.add, [("W1",), ("HI",)], [("QNF",)])
+        tt(T.YF[:], T.W2[:], T.YL[:], A_.add, [("W2",), ("YL",)], [("YF",)])
+        tcopy(T.QNO[:], T.QNF[:], [("QNF",)], [("QNO",)])
+        tcopy(T.YFO[:], T.YF[:], [("YF",)], [("YFO",)])
+        act(T.F1[:], T.BIG[:].indirect(T.QNO[:]), [BW, ("QNO",)], [("F1",)])
+        if not last:
+            ks = "KS%d" % t
+            tcopy(T[ks][:], T.PL[:].indirect(T.YFO[:]), [("PL",), ("YFO",)], [(ks,)])
+            send("K%d" % (t + 1), ks, "rk%d" % t)
+        blend(hs)
+        if not last:
+            send("H%d" % (t + 1), hs, "rh%d" % t)
+        codes("NL", "GO", "ABN")
+        if last:
+            tcopy(T.YB[:], T.NX[:].indirect(T.YFO[:]), [("NX",), ("YFO",)], [("YB",)])
+            dma("S", T.yb[:], T.YB[0:128:16, :], [("YB",)], [])
+            ts(T.YH[:], T[hs][:], -1026.0, None, A_.add, None, [(hs,)], [("YH",)])
+            dma("S", T.yh[:], T.YH[:], [("YH",)], [])
+        marks("ABN", range(0, 16), False, False, gm)
+        marks("ABY", range(3, 16), False, True, gm)
+        if t == 0:
+            nx_tables2()
+        ts(T.Z[:], T.CN[:, 0:256], 0.5, None, A_.is_gt, None, [("CN", 0, 256)], [("Z",)])
+        tt(T.SC[:], T.Z[:], T.DX[:], A_.mult, [("Z",), ("DX",)], [("SC",)])
+        tt(T.JC[:], T.JC[:], T.SC[:], A_.add, [("JC",), ("SC",)], [("JC",)])
+        if last:
+            tcopy(T.I1[:], T.JC[:], [("JC",)], [("I1",)])
+            ts(T.I2[:], T.I1[:], 255, None, A_.bitwise_and, None, [("I1",)], [("I2",)])
+            ts(T.I3[:], T.I1[:], 8, None, A_.arith_shift_right, None, [("I1",)], [("I3",)])
+            ts(T.SC[:], T.I2[:], 16.0, -2048.0, A_.mult, A_.add, [("I2",)], [("SC",)])
+            tt(T.J16[:], T.SC[:], T.I3[:], A_.add, [("SC",), ("I3",)], [("J16",)])
+        else:
+            ts(T.J16[:], T.JC[:], -2048.0, None, A_.add, None, [("JC",)], [("J16",)])
+        tcopy(T.LP[:], T.JC[:], [("JC",)], [("LP",)])
+        if not last:
+            tt(T.MSK[:], T.MSK[:], T.Z[:], A_.add, [("MSK",), ("Z",)], [("MSK",)])
+            ts(T.C16[:], T.MSK[:], 768.0, None, A_.mult, None, [("MSK",)], [("C16",)])
+
+        def fillj(i, r):
+            for e in range(2):
+                a = 2 * i + e
+                mm(T[r][:, 256 * e:256 * e + 256], T.BR[:, 128 * a:128 * a + 128], T.J16[:], True, True, [("BR",), ("J16",)], [(r, 256 * e, 256 * e + 256)], newgroup())
+
+        def evacj(i, r):
+            c = ("JR", 512 * i, 512 * i + 512)
+            if i % 2:
+                act(T.JR[:, c[1]:c[2]], T[r][:], [(r,)], [c], bias=2048.0)
+            else:
+                ts(T.JR[:, c[1]:c[2]], T[r][:], 2048.0, None, A_.add, None, [(r,)], [c])
+
+        ring_evac(8, fillj, evacj)
+        if last:
+            for j in range(4):
+                c = ("Q", 1024 * j, 1024 * j + 1024)
+                ind = T.JR[:].indirect(T.LP[:, 64 * j:64 * j + 64])
+                if j % 2:
+                    act(T.Q[:, c[1]:c[2]], ind, [("JR",), ("LP",)], [c])
+                else:
+                    tcopy(T.Q[:, c[1]:c[2]], ind, [("JR",), ("LP",)], [c])
+                dma("S", T.yj[:, c[1]:c[2]], T.Q[0:128:16, c[1]:c[2]], [c], [])
+            break
+        for j in range(2):
+            c = ("JH", 2048 * j, 2048 * j + 2048)
+            ts(T.JH[:, c[1]:c[2]], T.JR[:].indirect(T.LP[:, 128 * j:128 * j + 128]), -2048.0, None, A_.add, None, [("JR",), ("LP",)], [c])
+
+        def fillq(i, r):
+            gr = newgroup()
+            for e in range(2):
+                a = 2 * i + e
+                w = [(r, 256 * e, 256 * e + 256)]
+                o = T[r][:, 256 * e:256 * e + 256]
+                mm(o, T.IB[:], T.X[:, a:4096:16], True, False, [("IB",), ("X",)], w, gr)
+                mm(o, T.ZW[:], T.ZS[:, 256 * e:256 * e + 256], False, False, [("ZW",), ("ZS",)], w, gr)
+                mm(o, T.BR[:, 128 * a:128 * a + 128], T.C16[:], False, True, [("BR",), ("C16",)], w, gr)
+
+        def evacq(i, r):
+            c = ("Q", 512 * i, 512 * i + 512)
+            act(T.Q[:, c[1]:c[2]], T[r][:], [(r,)], [c], bias=1024.0 + 2 * i / 8192.0)
+
+        ring_evac(8, fillq, evacq)
+        pull(T.NX[:], ("NX",), "YFO", None)
+        tcopy(T.B16[:], T.SC[:, 15:256:16], [("SC",)], [("B16",)])
+        op("V", lambda: V.tensor_reduce(T.CNT[:, 0:1], T.MT[:], AxisListType.X, A_.add), [("MT",)], [("CNT", 0, 1)])
+        mm(T.SM[:, 16:17], T.BO[:], T.CNT[:, 0:1], True, True, [("BO",), ("CNT", 0, 1)], [("SM", 16, 17)], newgroup())
+        for j in range(2):
+            extract(128 * j, 128 * j + 128, j == 0)
+        ts(T.LP[:], T.KEY[:, 0:256], 2048.0, None, A_.add, None, [("KEY", 0, 256)], [("LP",)])
+        for j in range(4):
+            c = ("BIG", 1024 * j, 1024 * j + 1024)
+            ind = T.Q[:].indirect(T.LP[:, 64 * j:64 * j + 64])
+            if j % 2:
+                act(T.BIG[:, c[1]:c[2]], ind, [("Q",), ("LP",)], [c])
+            else:
+                tcopy(T.BIG[:, c[1]:c[2]], ind, [("Q",), ("LP",)], [c])
+        ts(T.JC[:], T.KEY[:, 0:256], 2048.0, None, A_.add, None, [("KEY", 0, 256)], [("JC",)])
+        tcopy(T.PJ[:, 0:1], T.SM[:, 16:17], [("SM", 16, 17)], [("PJ",)])
+        ts(T.PI[:, 0:1], T.PJ[:, 0:1], 31, None, A_.bitwise_and, None, [("PJ",)], [("PI",)])
+        ts(T.PC[:, 0:1], T.PI[:, 0:1], 16.0, None, A_.mult, None, [("PI",)], [("PC",)])
+        tt(T.THR[:, 0:1], T.PC[:, 0:1], T.TT[:, 0:1], A_.add, [("PC",), ("TT",)], [("THR",)])
+        arrive("K%d" % (t + 1), "rk%d" % t)
+        arrive("H%d" % (t + 1), "rh%d" % t)
+
+    for e in ("V", "A", "T"):
+        need("G", "c" + e, count[e])
+    need("G", "cG", count["G"])
+    for (s, v) in [(k[0], k[1]) for k in snap if k[0][0] == "d"]:
+        need("G", s, v)
+    for t in range(3):
+        need("G", "rk%d" % t, nprv)
+        need("G", "rh%d" % t, nprv)
+    need("G", "ls", sent[0])

@@ -3,7 +3,10 @@ from concourse.mybir import dt, AluOpType, AxisListType, ActivationFunctionType
 
 A_ = AluOpType
 F = ActivationFunctionType
-CHUNKS = [(0, 96), (96, 192), (192, 256)]
+CHUNKS = [(0, 64), (64, 128), (128, 192), (192, 256)]
+PICKS = [6, 1, 1, 1, 7]
+YV, YA = 3, 7
+QA = 10
 BIAS = 262144.0
 NV = 4
 NSLOT = 8
@@ -15,30 +18,32 @@ def _sb(n, d="float32", p=128):
 
 SCRATCH = {
     "BIG": _sb(8448), "X": _sb(4096, "bfloat16"), "NX": _sb(4096, "int32"), "PL": _sb(4096, "int32"),
-    "JH": _sb(4096, "float16"), "JR": _sb(4096), "Q": _sb(4096),
+    "JR": _sb(4096), "Q": _sb(4096),
     "S": ("sbuf", [128, 256, 16], "float16"), "RL": ("sbuf", [128, 256, 16], "float16"),
-    "ER2": _sb(2048, "float16"), "ERM": _sb(2048, "float16"), "EX": _sb(2048, "float16"), "BR": _sb(2048, "float16"),
+    "ERM": _sb(2048, "float16"), "EX": _sb(2048), "BR": _sb(2048, "bfloat16"), "IF": _sb(128), "SQ": _sb(256 * 4, "bfloat16"),
     "IB": _sb(128, "bfloat16"), "IH": _sb(128, "float16"), "BO": _sb(128), "BO8": _sb(8, "float16"),
     "APA": _sb(128, "bfloat16"), "IOB": _sb(256, "bfloat16"), "OH": _sb(16), "DM": _sb(256), "RS": _sb(256), "RM": _sb(256),
     "KC": _sb(256, "float16"), "CM": _sb(256, "float16"), "ZN": _sb(512, "float16"), "ZS": _sb(512, "float16"),
-    "ZW": _sb(128, "float16"), "LB": _sb(128), "T0": _sb(512), "T1": _sb(512), "PI": _sb(2, "int32"),
-    "PJ": _sb(2, "int32"), "FC": _sb(2), "GC": _sb(2), "FS": _sb(2), "PC": _sb(2),
+    "ZW": _sb(128, "float16"), "T0": _sb(512), "T1": _sb(512), "PI": _sb(2, "int32"),
+    "PJ": _sb(2, "int32"), "FC": _sb(2), "GC": _sb(2), "PB": _sb(2), "PC": _sb(2),
+    "NNI": _sb(256, "int32"), "NNF": _sb(256), "NNT": _sb(256), "SW": _sb(512),
     "KI": _sb(256, "int32"), "HB": _sb(256, "bfloat16"), "THI": _sb(2, "int32"), "THF": _sb(2), "BMI": _sb(256, "int32"),
-    "BMF": _sb(256), "TT": _sb(2), "THR": _sb(2), "TB": _sb(2),
+    "BMF": _sb(256), "TT": _sb(2), "THR": _sb(2),
     "K0": _sb(256, "uint16"), "K1": _sb(256, "uint16"), "K2": _sb(256, "uint16"), "K3": _sb(256, "uint16"),
     "H0": _sb(256, "float16"), "H1": _sb(256, "float16"), "H2": _sb(256, "float16"), "H3": _sb(256, "float16"),
     "KS0": _sb(256, "uint16"), "KS1": _sb(256, "uint16"), "KS2": _sb(256, "uint16"),
     "HS0": _sb(256, "float16"), "HS1": _sb(256, "float16"), "HS2": _sb(256, "float16"), "HS3": _sb(256, "float16"),
     "HA": _sb(256, "float16"),
     "PS": _sb(256), "SC": _sb(256), "Z": _sb(256), "F1": _sb(256), "SS": _sb(256), "S2": _sb(256, "float16"), "R2": _sb(256, "float16"),
-    "MT": _sb(16), "MKI": _sb(16, "int32"), "KWI": _sb(16, "int32"), "LI": _sb(16), "E1": _sb(16), "E2": _sb(16), "HI": _sb(16), "B16": _sb(16),
+    "MT": _sb(16), "MKI": _sb(16, "int32"), "KWI": _sb(16, "int32"), "LI": _sb(16), "E0": _sb(16), "E1": _sb(16), "E2": _sb(16), "HI": _sb(16), "B16": _sb(16),
     "U1": _sb(16), "U2": _sb(16), "QF": _sb(16), "QXF": _sb(16), "QO": _sb(16, "uint16"), "QXO": _sb(16, "uint16"),
     "VI": _sb(16, "int32"), "FR": _sb(16), "YL": _sb(16), "YO": _sb(16, "uint16"), "VL": _sb(16), "VO": _sb(16, "uint16"), "NL": _sb(16),
     "GO": _sb(16), "W1": _sb(16), "W2": _sb(16), "YF": _sb(16), "YFO": _sb(16, "uint16"), "QNF": _sb(16), "QNO": _sb(16, "uint16"),
     "WI": _sb(16, "int32"), "AB": _sb(32, "int32"), "ABY": _sb(32), "ABN": _sb(32), "Y16": _sb(16),
-    "LA": _sb(128 * NSLOT, "bfloat16"), "RB": _sb(256 * NSLOT, "bfloat16"),
-    "CNT": _sb(2), "MSK": _sb(256), "C16": _sb(256, "float16"), "DX": _sb(256), "JC": _sb(256), "J16": _sb(256, "float16"),
-    "LP": _sb(256, "uint16"), "I1": _sb(256, "int32"), "I2": _sb(256, "int32"), "I3": _sb(256, "int32"), "PSG": _sb(256),
+    "RY": _sb(256 * (16 - YV), "bfloat16"), "LA": _sb(128 * NSLOT, "bfloat16"), "RB": _sb(256 * NSLOT, "bfloat16"),
+    "CNT": _sb(2), "M16": _sb(256, "bfloat16"), "C16": _sb(256, "bfloat16"), "DX": _sb(256), "JC": _sb(256),
+    "JL": _sb(256, "bfloat16"), "JH": _sb(256, "bfloat16"),
+    "LP": _sb(256, "uint16"), "PSG": _sb(256), "ZZ": _sb(256),
     "YB": _sb(256), "YH": _sb(256, "bfloat16"),
     "R0": ("psum", [128, 512], "float32"), "R1": ("psum", [128, 512], "float32"),
     "R2P": ("psum", [128, 512], "float32"), "R3": ("psum", [128, 512], "float32"),
@@ -47,7 +52,7 @@ SCRATCH = {
 }
 RING = ["R0", "R1", "R2P", "R3"]
 PSUM = RING + ["KEY", "HP", "CN", "SM"]
-NDMA = 60
+NDMA = 40
 SEMAPHORES = ["cV", "cA", "cT", "cG"] + ["d%d" % i for i in range(NDMA)] + ["rh%d" % t for t in range(3)] + ["rk%d" % t for t in range(3)] + ["ls"]
 
 
@@ -111,14 +116,13 @@ def rank_program(g, core, T, topo):
         fn().then_inc(T.sem["c" + q], 1)
         note(q, reads, writes, "c" + q, count[q], group)
 
-    def dma(q, out, in_, reads, writes, ndep=1):
+    def dma(q, out, in_, reads, writes):
         deps(q, reads, writes, None)
         name = "d%d" % ndma[0]
         ndma[0] += 1
         queue[q].dma_start(out, in_).then_inc(T.sem[name], 16)
         note("dma", reads, writes, name, 16, None)
         snap[(name, 16)] = dict(known[q])
-        return name
 
     def dmas(q, pairs, writes):
         name = "d%d" % ndma[0]
@@ -132,8 +136,8 @@ def rank_program(g, core, T, topo):
     def tcopy(out, in_, r, w):
         op("V", lambda: V.tensor_copy(out, in_), r, w)
 
-    def tt(out, a, b, o, r, w):
-        op("V", lambda: V.tensor_tensor(out, a, b, o), r, w)
+    def tt(out, a, b, o, r, w, group=None):
+        op("V", lambda: V.tensor_tensor(out, a, b, o), r, w, group)
 
     def ts(out, a, s1, s2, o0, o1, r, w):
         if o1 is None:
@@ -141,8 +145,8 @@ def rank_program(g, core, T, topo):
         else:
             op("V", lambda: V.tensor_scalar(out, a, s1, s2, o0, o1), r, w)
 
-    def act(out, in_, r, w, bias=0.0, scale=1.0):
-        op("A", lambda: S_.activation(out, in_, F.Identity, bias=bias, scale=scale), r, w)
+    def act(out, in_, r, w, bias=0.0):
+        op("A", lambda: S_.activation(out, in_, F.Identity, bias=bias), r, w)
 
     def scan(out, d0, d1, o0, o1, r, w):
         op("V", lambda: V.tensor_tensor_scan(out, d0, d1, 0.0, o0, o1), r, w)
@@ -161,116 +165,105 @@ def rank_program(g, core, T, topo):
 
     dma("S", T.KI[:], T.kt[:], [], [("KI",)])
     dma("S", T.HB[:], T.hm[:], [], [("HB",)])
-    for j in range(4):
-        dma("S", T.X[:, 1024 * j:1024 * j + 1024], T.xp[:, 1024 * j:1024 * j + 1024], [], [("X", 1024 * j, 1024 * j + 1024)])
+    dma("A", T.NNI[:], T.nx[:], [], [("NNI",)])
     dma("A", T.THI[0:8, :], T.th[:], [], [("THI",)])
     dma("A", T.BMI[0:8, :], T.bm[:], [], [("BMI",)])
+    for j in range(4):
+        dma("S", T.X[:, 1024 * j:1024 * j + 1024], T.xp[:, 1024 * j:1024 * j + 1024], [], [("X", 1024 * j, 1024 * j + 1024)])
     dmas("S", [(T.NX[k:128:16, :], T.nx[:]) for k in range(16)], [("NX",)])
     dma("S", T.PL[:], T.pl[:], [], [("PL",)])
 
     op("G", lambda: g.iota(T.PI[:], [[0, 2]], 0, 1), [], [("PI",)])
-    iota(T.T0[:, 0:128], [[1, 8], [0, 16]], 0, 0, [("T0", 0, 128)])
-    iota(T.T0[:, 128:256], [[0, 8], [1, 16]], 0, 0, [("T0", 128, 256)])
-    iota(T.T1[:, 0:256], [[0, 16], [1, 16]], 0, 0, [("T1", 0, 256)])
-    iota(T.T1[:, 256:512], [[1, 256]], 0, 0, [("T1", 256, 512)])
     iota(T.T0[:, 256:384], [[1, 128]], 0, -1, [("T0", 256, 384)])
+    iota(T.T1[:, 256:512], [[1, 256]], 0, 0, [("T1", 256, 512)])
+    iota(T.T0[:, 0:128], [[1, 8], [0, 16]], 0, 0, [("T0", 0, 128)])
+    iota(T.T1[:, 0:256], [[0, 16], [1, 16]], 0, 0, [("T1", 0, 256)])
+    iota(T.T0[:, 128:256], [[0, 8], [1, 16]], 0, 0, [("T0", 128, 256)])
     iota(T.T0[0:8, 384:512], [[1, 8], [0, 16]], 0, -1, [("T0", 384, 512)])
     iota(T.B16[:], [[16, 16]], 0, 0, [("B16",)])
     ts(T.PJ[:], T.PI[:], 15, None, A_.bitwise_and, None, [("PI",)], [("PJ",)])
     tcopy(T.FC[:], T.PJ[:], [("PJ",)], [("FC",)])
     ts(T.PI[:], T.PI[:], 4, None, A_.arith_shift_right, None, [("PI",)], [("PI",)])
     tcopy(T.GC[:], T.PI[:], [("PI",)], [("GC",)])
-    ts(T.FS[:], T.FC[:], 256.0, None, A_.mult, None, [("FC",)], [("FS",)])
+    ts(T.PJ[:], T.PI[:], 1, None, A_.bitwise_and, None, [("PI",)], [("PJ",)])
+    tcopy(T.PB[:, 1:2], T.PJ[:, 1:2], [("PJ",)], [("PB", 1, 2)])
+    ts(T.PB[:, 0:1], T.PJ[:, 0:1], -1.0, 1.0, A_.mult, A_.add, [("PJ",)], [("PB", 0, 1)])
     fcol, gcol = T.FC[:, 0:1], T.GC[:, 0:1]
     tcopy(T.K0[:], T.KI[:], [("KI",)], [("K0",)])
     ts(T.H0[:], T.HB[:], 1026.0, None, A_.add, None, [("HB",)], [("H0",)])
-    ts(T.IB[:], T.T0[:, 256:384], 0.0, None, A_.is_equal, None, [("T0", 256, 384)], [("IB",)])
-    ts(T.IH[:], T.T0[:, 256:384], 0.0, None, A_.is_equal, None, [("T0", 256, 384)], [("IH",)])
-    ts(T.ZW[:], T.T0[:, 256:384], 0.0, 1.0 / 8192, A_.is_equal, A_.mult, [("T0", 256, 384)], [("ZW",)])
-    ts(T.ZN[:, 0:256], T.T1[:, 256:512], -256.0, None, A_.add, None, [("T1", 256, 512)], [("ZN", 0, 256)])
-    tcopy(T.ZN[:, 256:512], T.T1[:, 256:512], [("T1", 256, 512)], [("ZN", 256, 512)])
-
-    def ring_evac(n, fill, evac):
-        for i in range(n):
-            fill(i, RING[i % 4])
-            evac(i, RING[i % 4])
-
-    def fill0(i, r):
-        gr = newgroup()
-        mm(T[r][:], T.IB[:], T.X[:, 512 * i:512 * i + 512], True, False, [("IB",), ("X", 512 * i, 512 * i + 512)], [(r,)], gr)
-        mm(T[r][:], T.ZW[:], T.ZN[:], False, True, [("ZW",), ("ZN",)], [(r,)], gr)
-
-    def evac0(i, r):
-        b = 1024.0 + (512 * i + 256 - 2048) / 8192.0
-        w = [("BIG", 512 * i, 512 * i + 512)]
-        if i % 2:
-            act(T.BIG[:, 512 * i:512 * i + 512], T[r][:], [(r,)], w, bias=b)
-        else:
-            ts(T.BIG[:, 512 * i:512 * i + 512], T[r][:], b, None, A_.add, None, [(r,)], w)
-
-    ring_evac(8, fill0, evac0)
-
-    op("V", lambda: V.tensor_scalar(T.CM[:], T.T1[:, 0:256], 0.0, -1026.0, A_.mult, A_.add), [("T1", 0, 256)], [("CM",)])
+    mp = ("T0", 256, 384)
+    ts(T.IB[:], T.T0[:, 256:384], 0.0, None, A_.is_equal, None, [mp], [("IB",)])
+    ts(T.IH[:], T.T0[:, 256:384], 0.0, None, A_.is_equal, None, [mp], [("IH",)])
+    ts(T.ZW[:], T.T0[:, 256:384], 0.0, 1.0 / 8192, A_.is_equal, A_.mult, [mp], [("ZW",)])
+    col = ("T1", 256, 512)
+    ts(T.ZN[:, 0:256], T.T1[:, 256:512], -256.0, None, A_.add, None, [col], [("ZN", 0, 256)])
+    tcopy(T.ZN[:, 256:512], T.T1[:, 256:512], [col], [("ZN", 256, 512)])
+    ts(T.CM[:], T.T1[:, 0:256], 0.0, -1026.0, A_.mult, A_.add, [("T1", 0, 256)], [("CM",)])
     tcopy(T.KC[:], T.T1[:, 0:256], [("T1", 0, 256)], [("KC",)])
-    ts(T.BO8[:], T.T1[:, 256:264], gcol, 32.0, A_.is_equal, A_.mult, [("T1", 256, 512), ("GC",)], [("BO8",)])
+    ts(T.OH[:], T.T1[:, 256:272], fcol, None, A_.is_equal, None, [col, ("FC",)], [("OH",)])
+    ts(T.BO[:], T.T0[:, 0:128], gcol, None, A_.is_equal, None, [("T0", 0, 128), ("GC",)], [("BO",)])
+    for k in range(16):
+        op("A", lambda: S_.activation(T.BR[:, 128 * k:128 * k + 128], T.BO[:], F.Identity, scale=T.OH[:, k:k + 1]), [("BO",), ("OH",)], [("BR", 128 * k, 128 * k + 128)])
+    ts(T.BO8[:], T.T1[:, 256:264], gcol, -16.0, A_.is_equal, A_.mult, [col, ("GC",)], [("BO8",)])
     for r in range(4):
-        ts(T.ER2[:, 512 * r:512 * r + 512], T.T1[:], 0.0, None, A_.mult, None, [("T1",)], [("ER2", 512 * r, 512 * r + 512)])
+        ts(T.ERM[:, 512 * r:512 * r + 512], T.ZN[:], 0.0, None, A_.mult, None, [("ZN",)], [("ERM", 512 * r, 512 * r + 512)])
     for r in range(16):
-        tcopy(T.ER2[:, 128 * r + r:128 * r + 128:16], T.BO8[:], [("BO8",), ("ER2", 128 * r, 128 * r + 128)], [("ER2", 128 * r, 128 * r + 128)])
-    ts(T.ERM[:], T.ER2[:], -0.5, None, A_.mult, None, [("ER2",)], [("ERM",)])
-    ts(T.OH[:], T.T1[:, 256:272], fcol, None, A_.is_equal, None, [("T1", 256, 512), ("FC",)], [("OH",)])
+        e = ("ERM", 128 * r, 128 * r + 128)
+        tcopy(T.ERM[:, 128 * r + r:128 * r + 128:16], T.BO8[:], [("BO8",), e], [e])
     ts(T.DM[:], T.T1[:, 0:256], fcol, None, A_.is_equal, None, [("T1", 0, 256), ("FC",)], [("DM",)])
     ts(T.RS[:], T.T1[:, 0:256], 0.0, None, A_.is_gt, None, [("T1", 0, 256)], [("RS",)])
     ts(T.RM[:], T.RS[:], -2.0e9, 1.0e9, A_.mult, A_.add, [("RS",)], [("RM",)])
-    ts(T.BO[:], T.T0[:, 0:128], gcol, None, A_.is_equal, None, [("T0", 0, 128), ("GC",)], [("BO",)])
-    ts(T.LB[0:8, :], T.T0[0:8, 384:512], 0.0, None, A_.is_equal, None, [("T0", 384, 512)], [("LB",)])
+    ts(T.PS[0:8, 0:128], T.T0[0:8, 384:512], 0.0, None, A_.is_equal, None, [("T0", 384, 512)], [("PS",)])
     ts(T.LI[:], T.B16[:], fcol, None, A_.add, None, [("B16",), ("FC",)], [("LI",)])
     ts(T.HI[:], T.LI[:], 8192.0, None, A_.add, None, [("LI",)], [("HI",)])
     ts(T.E2[:], T.LI[:], 15.0, -4096.0, A_.mult, A_.add, [("LI",)], [("E2",)])
-    tcopy(T.THF[0:8, :], T.THI[0:8, :], [("THI",)], [("THF",)])
-    tcopy(T.BMF[0:8, :], T.BMI[0:8, :], [("BMI",)], [("BMF",)])
-    mm(T.SM[:, 0:2], T.LB[0:8, :], T.THF[0:8, :], True, True, [("LB",), ("THF",)], [("SM", 0, 2)], newgroup())
-    mm(T.SM[:, 256:512], T.LB[0:8, :], T.BMF[0:8, :], True, True, [("LB",), ("BMF",)], [("SM", 256, 512)], newgroup())
-    ts(T.TT[:], T.SM[:, 0:2], 16.0, -BIAS, A_.mult, A_.add, [("SM", 0, 2)], [("TT",)])
-    tcopy(T.THR[:], T.TT[:], [("TT",)], [("THR",)])
-    tt(T.Z[:], T.SM[:, 256:512], T.DM[:], A_.mult, [("SM", 256, 512), ("DM",)], [("Z",)])
-    scan(T.SC[:], T.RS[:], T.Z[:], A_.mult, A_.add, [("RS",), ("Z",)], [("SC",)])
-    tcopy(T.B16[:], T.SC[:, 15:256:16], [("SC",)], [("B16",)])
+    tt(T.E0[:], T.HI[:], T.E2[:], A_.add, [("HI",), ("E2",)], [("E0",)])
+
+    for i in range(8):
+        r = RING[i % 4]
+        gr = newgroup()
+        c = ("BIG", 512 * i, 512 * i + 512)
+        mm(T[r][:], T.IB[:], T.X[:, 512 * i:512 * i + 512], True, False, [("IB",), ("X", 512 * i, 512 * i + 512)], [(r,)], gr)
+        mm(T[r][:], T.ZW[:], T.ZN[:], False, True, [("ZW",), ("ZN",)], [(r,)], gr)
+        b = 1024.0 + (512 * i + 256 - 2048) / 8192.0
+        if i % 2:
+            act(T.BIG[:, c[1]:c[2]], T[r][:], [(r,)], [c], bias=b)
+        else:
+            ts(T.BIG[:, c[1]:c[2]], T[r][:], b, None, A_.add, None, [(r,)], [c])
 
     def setup_late():
+        tcopy(T.THF[0:8, :], T.THI[0:8, :], [("THI",)], [("THF",)])
+        tcopy(T.BMF[0:8, :], T.BMI[0:8, :], [("BMI",)], [("BMF",)])
+        mm(T.SM[:, 0:2], T.PS[0:8, 0:128], T.THF[0:8, :], True, True, [("PS",), ("THF",)], [("SM", 0, 2)], newgroup())
+        mm(T.SM[:, 256:512], T.PS[0:8, 0:128], T.BMF[0:8, :], True, True, [("PS",), ("BMF",)], [("SM", 256, 512)], newgroup())
+        ts(T.TT[:], T.SM[:, 0:2], 16.0, BIAS, A_.mult, A_.add, [("SM", 0, 2)], [("TT",)])
+        tcopy(T.THR[:], T.TT[:], [("TT",)], [("THR",)])
+        tt(T.Z[:], T.SM[:, 256:512], T.DM[:], A_.mult, [("SM", 256, 512), ("DM",)], [("Z",)])
+        scan(T.SC[:], T.RS[:], T.Z[:], A_.mult, A_.add, [("RS",), ("Z",)], [("SC",)])
+        tcopy(T.B16[:], T.SC[:, 15:256:16], [("SC",)], [("B16",)])
         ts(T.APA[:], T.T0[:, 128:256], 1.0, None, A_.add, None, [("T0", 128, 256)], [("APA",)])
         tt(T.APA[:], T.APA[:], T.BO[:], A_.mult, [("APA",), ("BO",)], [("APA",)])
         ts(T.APA[:], T.APA[:], -1.0, None, A_.add, None, [("APA",)], [("APA",)])
-        ts(T.IOB[:], T.T1[:, 256:512], 1.0, None, A_.add, None, [("T1", 256, 512)], [("IOB",)])
-        for k in range(16):
-            c = (128 * k, 128 * k + 128)
-            ts(T.EX[:, c[0]:c[1]], T.IH[:], T.OH[:, k:k + 1], None, A_.mult, None, [("IH",), ("OH",)], [("EX",) + c])
-            ts(T.BR[:, c[0]:c[1]], T.BO[:], T.OH[:, k:k + 1], None, A_.mult, None, [("BO",), ("OH",)], [("BR",) + c])
-        ts(T.ZS[:, 0:256], T.T1[:, 256:512], 16.0, -2048.0, A_.mult, A_.add, [("T1", 256, 512)], [("ZS", 0, 256)])
-        ts(T.ZS[:, 256:512], T.T1[:, 256:512], 16.0, -2047.0, A_.mult, A_.add, [("T1", 256, 512)], [("ZS", 256, 512)])
-        ts(T.PSG[:], T.T1[:, 256:512], T.FS[:, 0:1], None, A_.add, None, [("T1", 256, 512), ("FS",)], [("PSG",)])
-        tcopy(T.JC[:], T.PSG[:], [("PSG",)], [("JC",)])
-        op("V", lambda: V.memset(T.MSK[:], 0.0), [], [("MSK",)])
+        ts(T.IOB[:], T.T1[:, 256:512], 1.0, None, A_.add, None, [col], [("IOB",)])
 
-    def extract(lo, hi, first):
+    def setup_last():
+        tcopy(T.NNF[:], T.NNI[:], [("NNI",)], [("NNF",)])
+        op("V", lambda: V.transpose(T.NNT[:], T.NNF[:]), [("NNF",)], [("NNT",)])
+        for be in range(2):
+            for ga in range(2):
+                w = 128 * (2 * be + ga)
+                ts(T.SW[:, w:w + 128], T.T0[:, 256:384], float(16 * (ga - be)), T.PB[:, be:be + 1], A_.is_equal, A_.mult, [mp, ("PB",)], [("SW", w, w + 128)])
         gr = newgroup()
-        for k in range(16):
-            mm(T.KEY[:, lo:hi], T.EX[:, 128 * k:128 * k + 128], T.JH[:, 16 * lo + k:16 * hi:16], k == 0, k == 15,
-               [("EX",), ("JH", 16 * lo, 16 * hi)], [("KEY", lo, hi)], gr)
-
-    def nx_tables():
-        for j in range(4):
-            c = (1024 * j, 1024 * j + 1024)
-            ts(T.JH[:, c[0]:c[1]], T.NX[:, c[0]:c[1]], -2048.0, None, A_.add, None, [("NX",) + c], [("JH",) + c])
-
-    def nx_tables2():
-        extract(0, 256, True)
-        ts(T.I1[:], T.KEY[:, 0:256], 2048.0, None, A_.add, None, [("KEY", 0, 256)], [("I1",)])
-        ts(T.I2[:], T.I1[:], 15, None, A_.bitwise_and, None, [("I1",)], [("I2",)])
-        ts(T.I3[:], T.I1[:], 4, None, A_.arith_shift_right, None, [("I1",)], [("I3",)])
-        ts(T.DX[:], T.I2[:], 256.0, None, A_.mult, None, [("I2",)], [("DX",)])
-        tt(T.DX[:], T.DX[:], T.I3[:], A_.add, [("DX",), ("I3",)], [("DX",)])
-        tt(T.DX[:], T.DX[:], T.PSG[:], A_.subtract, [("DX",), ("PSG",)], [("DX",)])
+        for be in range(2):
+            for b in range(8):
+                for ga in range(2):
+                    w = 128 * (2 * be + ga)
+                    mm(T.KEY[:, 2 * b + be:256:16], T.SW[:, w:w + 128], T.NNT[:, 32 * b + 16 * ga:32 * b + 16 * ga + 16], ga == 0, ga == 1,
+                       [("SW", w, w + 128), ("NNT",)], [("KEY", 0, 256)], gr)
+        ts(T.PSG[:], T.T1[:, 256:512], 16.0, fcol, A_.mult, A_.add, [col, ("FC",)], [("PSG",)])
+        ts(T.IF[:], T.T0[:, 256:384], 0.0, None, A_.is_equal, None, [mp], [("IF",)])
+        ts(T.ZS[:, 0:256], T.T1[:, 256:512], 16.0, -2048.0, A_.mult, A_.add, [col], [("ZS", 0, 256)])
+        ts(T.ZS[:, 256:512], T.T1[:, 256:512], 16.0, -2047.0, A_.mult, A_.add, [col], [("ZS", 256, 512)])
 
     BW = ("BIG", 0, 8448)
     nslot = [0]
@@ -281,6 +274,27 @@ def rank_program(g, core, T, topo):
         ts(T.AB[:, 0:16], T.WI[:], 15, None, A_.bitwise_and, None, [("WI",)], [("AB", 0, 16)])
         ts(T.AB[:, 16:32], T.WI[:], 4, None, A_.arith_shift_right, None, [("WI",)], [("AB", 16, 32)])
         tcopy(T[dst][:], T.AB[:], [("AB",)], [(dst,)])
+
+    def scalar_codes(src, cols):
+        for c in cols:
+            s = c % 4
+            sq, rb = ("SQ", 256 * s, 256 * s + 256), ("RY", 256 * (c - YV), 256 * (c - YV) + 256)
+            op("A", lambda: S_.activation(T.SQ[:, sq[1]:sq[2]], T.IOB[:], F.Square, bias=T[src][:, 16 + c:17 + c], scale=-1.0), [("IOB",), (src,)], [sq])
+            if c > cols[0]:
+                relu_codes(c - 1)
+        relu_codes(cols[-1])
+
+    def relu_codes(c):
+        sq, rb = ("SQ", 256 * (c % 4), 256 * (c % 4) + 256), ("RY", 256 * (c - YV), 256 * (c - YV) + 256)
+        op("A", lambda: S_.activation(T.RY[:, rb[1]:rb[2]], T.SQ[:, sq[1]:sq[2]], F.Relu, bias=1.0, scale=-1.0), [sq], [rb])
+
+    def scalar_marks(src, cols, gr):
+        for c in cols:
+            s = nslot[0] % NSLOT
+            nslot[0] += 1
+            la, rb = ("LA", 128 * s, 128 * s + 128), ("RY", 256 * (c - YV), 256 * (c - YV) + 256)
+            ts(T.LA[:, la[1]:la[2]], T.APA[:], T[src][:, c:c + 1], None, A_.is_equal, None, [("APA",), (src,)], [la])
+            mm(T.CN[:, 0:256], T.LA[:, la[1]:la[2]], T.RY[:, rb[1]:rb[2]], False, c == 15, [la, rb], [("CN", 0, 256)], gr)
 
     def marks(src, cols, first, last, gr):
         for c in cols:
@@ -297,7 +311,7 @@ def rank_program(g, core, T, topo):
         mm(T.HP[:, 0:256], T.IH[:], T.CM[:], False, True, [("IH",), ("CM",)], [("HP", 0, 256)], gr)
         act(T.BIG[:, 8192:8448], T.HP[:, 0:256], [("HP", 0, 256)], [("BIG", 8192, 8448)], bias=1024.0)
 
-    def pull(win, wr, off, dst):
+    def pull(win, wr, off):
         tt(T.Z[:], win.indirect(T[off][:]), T.DM[:], A_.mult, [wr, (off,), ("DM",)], [("Z",)])
         scan(T.SC[:], T.RS[:], T.Z[:], A_.mult, A_.add, [("RS",), ("Z",)], [("SC",)])
 
@@ -309,6 +323,23 @@ def rank_program(g, core, T, topo):
     def blend(out):
         tt(T.SS[:], T.F1[:], T.HP[:, 0:256], A_.add, [("F1",), ("HP", 0, 256)], [("SS",)])
         ts(T[out][:], T.SS[:], 0.5, 513.75, A_.mult, A_.add, [("SS",)], [(out,)])
+
+    picked = [16, 0]
+
+    def picks(n):
+        for k in range(picked[0], min(16, picked[0] + n)):
+            mm(T.CN[:, 256:512], T.EX[:, 128 * k:128 * k + 128], T.BIG[:, k:4096:16], k == 0, k == 15,
+               [("EX", 128 * k, 128 * k + 128), ("BIG", 0, 4096)], [("CN", 256, 512)], picked[1])
+            picked[0] = k + 1
+
+    def halves(out, src, off, srcs):
+        for j in range(4):
+            c = (out, 1024 * j, 1024 * j + 1024)
+            ind = T[src][:, 0:4096].indirect(T[off][:, 64 * j:64 * j + 64])
+            if j % 2:
+                act(T[out][:, c[1]:c[2]], ind, srcs + [(off,)], [c])
+            else:
+                tcopy(T[out][:, c[1]:c[2]], ind, srcs + [(off,)], [c])
 
     nxt = T.cores[(rank + 1) % len(T.cores)]
     mask = topo.mask(core, nxt)
@@ -326,173 +357,192 @@ def rank_program(g, core, T, topo):
     def arrive(dst, sem):
         note("remote", [], [(dst,)], sem, nprv, None)
 
+    def qfill(i):
+        r = RING[i % 4]
+        gr = newgroup()
+        mm(T[r][:], T.ZW[:], T.ZS[:], True, False, [("ZW",), ("ZS",)], [(r,)], gr)
+        for e in range(2):
+            a = 2 * i + e
+            mm(T[r][:, 256 * e:256 * e + 256], T.IB[:], T.X[:, a:4096:16], False, False, [("IB",), ("X",)], [(r,)], gr)
+            if t:
+                mm(T[r][:, 256 * e:256 * e + 256], T.BR[:, 128 * a:128 * a + 128], T.C16[:], False, False, [("BR",), ("C16",)], [(r,)], gr)
+        return gr
+
+    def qmark(i, gr):
+        r = RING[i % 4]
+        for e in range(2):
+            a = 2 * i + e
+            mm(T[r][:, 256 * e:256 * e + 256], T.BR[:, 128 * a:128 * a + 128], T.M16[:], False, e == 1, [("BR",), ("M16",)], [(r,)], gr)
+        for e in range(2):
+            a = 2 * i + e
+            act(T.Q[:, a:4096:16], T[r][:, 256 * e:256 * e + 256], [(r,)], [("Q%d" % a,)], bias=1024.0 + 2 * i / 8192.0)
+
     for t in range(NV):
         last = t == NV - 1
         kb, hb, hs = "K%d" % t, "H%d" % t, "HS%d" % t
+        if t:
+            picked[0], picked[1] = 0, newgroup()
         to_hp(hb)
         for (l0, l1) in CHUNKS:
             xc = ("BIG", 4096 + 16 * l0, 4096 + 16 * l1)
             act(T.BIG[:, xc[1]:xc[2]], T.BIG[:, 0:4096].indirect(T[kb][:, l0:l1]), [("BIG", 0, 4096), (kb,)], [xc])
         if t == 0:
             setup_late()
-            nx_tables()
-        tt(T.E1[:], T.HI[:], T.E2[:], A_.add, [("HI",), ("E2",)], [("E1",)])
-        tt(T.E1[:], T.E1[:], T.B16[:], A_.subtract, [("E1",), ("B16",)], [("E1",)])
+        else:
+            pull(T.NX[:], ("NX",), "YFO")
+            tcopy(T.B16[:], T.SC[:, 15:256:16], [("SC",)], [("B16",)])
+            ts(T.PI[:, 0:1], T.PJ[:, 0:1], 31, None, A_.bitwise_and, None, [("PJ",)], [("PI",)])
+            ts(T.PC[:, 0:1], T.PI[:, 0:1], 16.0, None, A_.mult, None, [("PI",)], [("PC",)])
+            tt(T.THR[:, 0:1], T.PC[:, 0:1], T.TT[:, 0:1], A_.add, [("PC",), ("TT",)], [("THR",)])
+            if t == 1:
+                tcopy(T.C16[:], T.M16[:], [("M16",)], [("C16",)])
+            elif not last:
+                tt(T.C16[:], T.C16[:], T.M16[:], A_.add, [("C16",), ("M16",)], [("C16",)])
+        tt(T.E1[:], T.E0[:], T.B16[:], A_.subtract, [("E0",), ("B16",)], [("E1",)])
         kgr = newgroup()
-        for (l0, l1) in CHUNKS:
+        for n, (l0, l1) in enumerate(CHUNKS):
             s3 = ("S", 16 * l0, 16 * l1)
             r3 = ("RL", 16 * l0, 16 * l1)
             ko = ("KEY", l0, l1)
+            a = 4096 + 16 * l0
             for k in range(16):
-                a = 4096 + 16 * l0
-                op("V", lambda k=k, a=a: V.tensor_tensor(T.S[:, l0:l1, k], T.BIG[:, a + k:4096 + 16 * l1:16], T.HP[:, l0:l1], A_.subtract),
+                tt(T.S[:, l0:l1, k], T.BIG[:, a + k:4096 + 16 * l1:16], T.HP[:, l0:l1], A_.subtract,
                    [("BIG", a, 4096 + 16 * l1), ("HP", 0, 256)], [s3], "s%d_%d" % (t, l0))
-            ts(T.RL[:, l0:l1, :], T.S[:, l0:l1, :], -1024.0, 0.0, A_.add, A_.max, [s3], [r3])
+            ts(T.RL[:, l0:l1, :], T.S[:, l0:l1, :], -2.0, -2048.0, A_.mult, A_.min, [s3], [r3])
+            picks(PICKS[n])
             mm(T.KEY[:, l0:l1], T.IH[:], T.KC[:, l0:l1], True, False, [("IH",), ("KC",)], [ko], kgr)
             for r in range(16):
                 mm(T.KEY[:, l0:l1], T.ERM[:, 128 * r:128 * r + 128], T.S[:, l0 + r:l1:16, :], False, False, [("ERM",), s3], [ko], kgr)
             for r in range(16):
-                mm(T.KEY[:, l0:l1], T.ER2[:, 128 * r:128 * r + 128], T.RL[:, l0 + r:l1:16, :], False, r == 15, [("ER2",), r3], [ko], kgr)
+                mm(T.KEY[:, l0:l1], T.ERM[:, 128 * r:128 * r + 128], T.RL[:, l0 + r:l1:16, :], False, r == 15, [("ERM",), r3], [ko], kgr)
+        picks(PICKS[-1])
         scan(T.PS[:], T.RM[:], T.KEY[:, 0:256], A_.max, A_.min, [("RM",), ("KEY", 0, 256)], [("PS",)])
         mk = T.PS[:, 15:256:16]
         tcopy(T.MKI[:], mk, [("PS",)], [("MKI",)])
         ts(T.MT[:], mk, T.THR[:, 0:1], None, A_.is_lt, None, [("PS",), ("THR",)], [("MT",)])
         ts(T.KWI[:], T.MKI[:], 15, None, A_.bitwise_and, None, [("MKI",)], [("KWI",)])
-        tt(T.U2[:], T.KWI[:], T.E2[:], A_.add, [("KWI",), ("E2",)], [("U2",)])
         tt(T.U1[:], T.KWI[:], T.E1[:], A_.add, [("KWI",), ("E1",)], [("U1",)])
-        tt(T.U2[:], T.U2[:], T.MT[:], A_.mult, [("U2",), ("MT",)], [("U2",)])
+        tt(T.U2[:], T.KWI[:], T.E2[:], A_.add, [("KWI",), ("E2",)], [("U2",)])
         tt(T.U1[:], T.U1[:], T.MT[:], A_.mult, [("U1",), ("MT",)], [("U1",)])
-        tt(T.QXF[:], T.U2[:], T.HI[:], A_.add, [("U2",), ("HI",)], [("QXF",)])
+        tt(T.U2[:], T.U2[:], T.MT[:], A_.mult, [("U2",), ("MT",)], [("U2",)])
         tt(T.QF[:], T.U1[:], T.B16[:], A_.add, [("U1",), ("B16",)], [("QF",)])
-        tcopy(T.QXO[:], T.QXF[:], [("QXF",)], [("QXO",)])
+        tt(T.QXF[:], T.U2[:], T.HI[:], A_.add, [("U2",), ("HI",)], [("QXF",)])
         tcopy(T.QO[:], T.QF[:], [("QF",)], [("QO",)])
+        tcopy(T.QXO[:], T.QXF[:], [("QXF",)], [("QXO",)])
         act(T.F1[:], T.BIG[:].indirect(T.QXO[:]), [BW, ("QXO",)], [("F1",)])
-        pull(T.BIG[:], BW, "QO", None)
+        pull(T.BIG[:], BW, "QO")
         place("YL")
         tcopy(T.YO[:], T.YL[:], [("YL",)], [("YO",)])
-        pull(T.NX[:], ("NX",), "YO", None)
+        pull(T.NX[:], ("NX",), "YO")
         tcopy(T.VO[:], T.SC[:, 15:256:16], [("SC",)], [("VO",)])
         tcopy(T.VL[:], T.SC[:, 15:256:16], [("SC",)], [("VL",)])
         blend("HA")
         act(T.F1[:], T.BIG[:, 0:4096].indirect(T.VO[:]), [("BIG", 0, 4096), ("VO",)], [("F1",)])
         to_hp("HA")
-        pull(T.BIG[:, 0:4096], ("BIG", 0, 4096), "VO", None)
+        pull(T.BIG[:, 0:4096], ("BIG", 0, 4096), "VO")
         tt(T.S2[:], T.F1[:], T.HP[:, 0:256], A_.subtract, [("F1",), ("HP", 0, 256)], [("S2",)])
-        ts(T.R2[:], T.S2[:], -1024.0, 0.0, A_.add, A_.max, [("S2",)], [("R2",)])
+        ts(T.R2[:], T.S2[:], -2.0, -2048.0, A_.mult, A_.min, [("S2",)], [("R2",)])
         g2 = newgroup()
         for r in range(16):
             mm(T.SM[:, 0:16], T.ERM[:, 128 * r:128 * r + 128], T.S2[:, r:256:16], r == 0, False, [("ERM",), ("S2",)], [("SM", 0, 16)], g2)
         for r in range(16):
-            mm(T.SM[:, 0:16], T.ER2[:, 128 * r:128 * r + 128], T.R2[:, r:256:16], False, r == 15, [("ER2",), ("R2",)], [("SM", 0, 16)], g2)
+            mm(T.SM[:, 0:16], T.ERM[:, 128 * r:128 * r + 128], T.R2[:, r:256:16], False, r == 15, [("ERM",), ("R2",)], [("SM", 0, 16)], g2)
+        picks(16)
         place("NL")
         tt(T.W1[:], T.VL[:], T.HI[:], A_.subtract, [("VL",), ("HI",)], [("W1",)])
         tt(T.W2[:], T.NL[:], T.YL[:], A_.subtract, [("NL",), ("YL",)], [("W2",)])
         codes("YL", "MT", "ABY")
         gm = newgroup()
-        marks("ABY", range(0, 3), True, False, gm)
+        scalar_codes("ABY", range(YV, YA))
+        if t:
+            tcopy(T.NNI[:], T.CN[:, 256:512], [("CN", 256, 512)], [("NNI",)])
+            qg = [] if last else [qfill(i) for i in range(4)]
         ts(T.GO[:], T.SM[:, 0:16], T.TT[:, 1:2], None, A_.is_le, None, [("SM", 0, 16), ("TT",)], [("GO",)])
         tt(T.GO[:], T.GO[:], T.MT[:], A_.mult, [("GO",), ("MT",)], [("GO",)])
-        tt(T.W1[:], T.W1[:], T.GO[:], A_.mult, [("W1",), ("GO",)], [("W1",)])
         tt(T.W2[:], T.W2[:], T.GO[:], A_.mult, [("W2",), ("GO",)], [("W2",)])
-        tt(T.QNF[:], T.W1[:], T.HI[:], A_.add, [("W1",), ("HI",)], [("QNF",)])
+        tt(T.W1[:], T.W1[:], T.GO[:], A_.mult, [("W1",), ("GO",)], [("W1",)])
         tt(T.YF[:], T.W2[:], T.YL[:], A_.add, [("W2",), ("YL",)], [("YF",)])
-        tcopy(T.QNO[:], T.QNF[:], [("QNF",)], [("QNO",)])
+        tt(T.QNF[:], T.W1[:], T.HI[:], A_.add, [("W1",), ("HI",)], [("QNF",)])
         tcopy(T.YFO[:], T.YF[:], [("YF",)], [("YFO",)])
+        tcopy(T.QNO[:], T.QNF[:], [("QNF",)], [("QNO",)])
         act(T.F1[:], T.BIG[:].indirect(T.QNO[:]), [BW, ("QNO",)], [("F1",)])
         if not last:
             ks = "KS%d" % t
             tcopy(T[ks][:], T.PL[:].indirect(T.YFO[:]), [("PL",), ("YFO",)], [(ks,)])
             send("K%d" % (t + 1), ks, "rk%d" % t)
+        scalar_codes("ABY", range(YA, 16))
+        if t:
+            tt(T.BMF[:], T.CN[:, 256:512], T.NNI[:], A_.subtract, [("CN", 256, 512), ("NNI",)], [("BMF",)])
+        codes("NL", "GO", "ABN")
+        marks("ABY", range(0, YV), True, False, gm)
+        if t == 0:
+            setup_last()
+            qg = [qfill(i) for i in range(4)]
+            for k in range(16):
+                op("A", lambda: S_.activation(T.EX[:, 128 * k:128 * k + 128], T.IF[:], F.Identity, scale=T.OH[:, k:k + 1]), [("IF",), ("OH",)], [("EX", 128 * k, 128 * k + 128)])
+        if not last:
+            op("V", lambda: V.tensor_reduce(T.CNT[:, 0:1], T.MT[:], AxisListType.X, A_.add), [("MT",)], [("CNT", 0, 1)])
+            mm(T.SM[:, 16:17], T.BO[:], T.CNT[:, 0:1], True, True, [("BO",), ("CNT", 0, 1)], [("SM", 16, 17)], newgroup())
+        marks("ABN", range(0, 6), False, False, gm)
         blend(hs)
         if not last:
             send("H%d" % (t + 1), hs, "rh%d" % t)
-        codes("NL", "GO", "ABN")
-        if last:
-            tcopy(T.YB[:], T.NX[:].indirect(T.YFO[:]), [("NX",), ("YFO",)], [("YB",)])
-            dma("S", T.yb[:], T.YB[0:128:16, :], [("YB",)], [])
-            ts(T.YH[:], T[hs][:], -1026.0, None, A_.add, None, [(hs,)], [("YH",)])
-            dma("S", T.yh[:], T.YH[:], [("YH",)], [])
-        marks("ABN", range(0, 16), False, False, gm)
-        marks("ABY", range(3, 16), False, True, gm)
-        if t == 0:
-            nx_tables2()
-        ts(T.Z[:], T.CN[:, 0:256], 0.5, None, A_.is_gt, None, [("CN", 0, 256)], [("Z",)])
-        tt(T.SC[:], T.Z[:], T.DX[:], A_.mult, [("Z",), ("DX",)], [("SC",)])
-        tt(T.JC[:], T.JC[:], T.SC[:], A_.add, [("JC",), ("SC",)], [("JC",)])
-        if last:
-            tcopy(T.I1[:], T.JC[:], [("JC",)], [("I1",)])
-            ts(T.I2[:], T.I1[:], 255, None, A_.bitwise_and, None, [("I1",)], [("I2",)])
-            ts(T.I3[:], T.I1[:], 8, None, A_.arith_shift_right, None, [("I1",)], [("I3",)])
-            ts(T.SC[:], T.I2[:], 16.0, -2048.0, A_.mult, A_.add, [("I2",)], [("SC",)])
-            tt(T.J16[:], T.SC[:], T.I3[:], A_.add, [("SC",), ("I3",)], [("J16",)])
-        else:
-            ts(T.J16[:], T.JC[:], -2048.0, None, A_.add, None, [("JC",)], [("J16",)])
-        tcopy(T.LP[:], T.JC[:], [("JC",)], [("LP",)])
+        marks("ABN", range(6, 16), False, False, gm)
+        if t:
+            ts(T.JC[:], T.BMF[:], 8192.0, 2048.0, A_.mult, A_.add, [("BMF",)], [("JC",)])
+        scalar_marks("ABY", range(YV, 16), gm)
         if not last:
-            tt(T.MSK[:], T.MSK[:], T.Z[:], A_.add, [("MSK",), ("Z",)], [("MSK",)])
-            ts(T.C16[:], T.MSK[:], 768.0, None, A_.mult, None, [("MSK",)], [("C16",)])
-
-        def fillj(i, r):
-            for e in range(2):
-                a = 2 * i + e
-                mm(T[r][:, 256 * e:256 * e + 256], T.BR[:, 128 * a:128 * a + 128], T.J16[:], True, True, [("BR",), ("J16",)], [(r, 256 * e, 256 * e + 256)], newgroup())
-
-        def evacj(i, r):
-            c = ("JR", 512 * i, 512 * i + 512)
-            if i % 2:
-                act(T.JR[:, c[1]:c[2]], T[r][:], [(r,)], [c], bias=2048.0)
-            else:
-                ts(T.JR[:, c[1]:c[2]], T[r][:], 2048.0, None, A_.add, None, [(r,)], [c])
-
-        ring_evac(8, fillj, evacj)
+            tcopy(T.PJ[:, 0:1], T.SM[:, 16:17], [("SM", 16, 17)], [("PJ",)])
+            ts(T.M16[:], T.CN[:, 0:256], 0.5, 768.0, A_.is_gt, A_.mult, [("CN", 0, 256)], [("M16",)])
+        if t == 0:
+            tt(T.DX[:], T.KEY[:, 0:256], T.PSG[:], A_.subtract, [("KEY", 0, 256), ("PSG",)], [("DX",)])
+        ts(T.ZZ[:], T.CN[:, 0:256], 0.5, None, A_.is_gt, None, [("CN", 0, 256)], [("ZZ",)])
+        tt(T.ZZ[:], T.ZZ[:], T.DX[:], A_.mult, [("ZZ",), ("DX",)], [("ZZ",)])
+        jold = "JC" if t else "PSG"
+        tt(T.JC[:], T[jold][:], T.ZZ[:], A_.add, [(jold,), ("ZZ",)], [("JC",)])
         if last:
+            tcopy(T.NNI[:], T.JC[:], [("JC",)], [("NNI",)])
+            ts(T.KI[:], T.NNI[:], 63, None, A_.bitwise_and, None, [("NNI",)], [("KI",)])
+            tcopy(T.JL[:], T.KI[:], [("KI",)], [("JL",)])
+            tt(T.JH[:], T.JC[:], T.KI[:], A_.subtract, [("JC",), ("KI",)], [("JH",)])
+        tcopy(T.LP[:], T.JC[:], [("JC",)], [("LP",)])
+        if last:
+            for i in range(8):
+                r = RING[i % 4]
+                for e in range(2):
+                    a = 2 * i + e
+                    for n, j in enumerate(("JL", "JH")):
+                        mm(T[r][:, 256 * e:256 * e + 256], T.BR[:, 128 * a:128 * a + 128], T[j][:], n == 0, n == 1, [("BR",), (j,)], [(r, 256 * e, 256 * e + 256)], ("j", i))
+                for e in range(2):
+                    a = 2 * i + e
+                    if i % 2:
+                        op("A", lambda: S_.activation(T.JR[:, a:4096:16], T[r][:, 256 * e:256 * e + 256], F.Copy), [(r,)], [("JR",)], "jr")
+                    else:
+                        op("V", lambda: V.tensor_copy(T.JR[:, a:4096:16], T[r][:, 256 * e:256 * e + 256]), [(r,)], [("JR",)], "jr")
+            halves("Q", "JR", "LP", [("JR",)])
+            tcopy(T.YB[:], T.NX[:].indirect(T.YFO[:]), [("NX",), ("YFO",)], [("YB",)])
+            ts(T.YH[:], T[hs][:], -1026.0, None, A_.add, None, [(hs,)], [("YH",)])
+            dma("S", T.yb[:], T.YB[0:128:16, :], [("YB",)], [])
+            dma("S", T.yh[:], T.YH[:], [("YH",)], [])
             for j in range(4):
-                c = ("Q", 1024 * j, 1024 * j + 1024)
-                ind = T.JR[:].indirect(T.LP[:, 64 * j:64 * j + 64])
-                if j % 2:
-                    act(T.Q[:, c[1]:c[2]], ind, [("JR",), ("LP",)], [c])
-                else:
-                    tcopy(T.Q[:, c[1]:c[2]], ind, [("JR",), ("LP",)], [c])
-                dma("S", T.yj[:, c[1]:c[2]], T.Q[0:128:16, c[1]:c[2]], [c], [])
+                c = (1024 * j, 1024 * j + 1024)
+                dma("S", T.yj[:, c[0]:c[1]], T.Q[0:128:16, c[0]:c[1]], [("Q",) + c], [])
             break
-        for j in range(2):
-            c = ("JH", 2048 * j, 2048 * j + 2048)
-            ts(T.JH[:, c[1]:c[2]], T.JR[:].indirect(T.LP[:, 128 * j:128 * j + 128]), -2048.0, None, A_.add, None, [("JR",), ("LP",)], [c])
-
-        def fillq(i, r):
-            gr = newgroup()
-            for e in range(2):
-                a = 2 * i + e
-                w = [(r, 256 * e, 256 * e + 256)]
-                o = T[r][:, 256 * e:256 * e + 256]
-                mm(o, T.IB[:], T.X[:, a:4096:16], True, False, [("IB",), ("X",)], w, gr)
-                mm(o, T.ZW[:], T.ZS[:, 256 * e:256 * e + 256], False, False, [("ZW",), ("ZS",)], w, gr)
-                mm(o, T.BR[:, 128 * a:128 * a + 128], T.C16[:], False, True, [("BR",), ("C16",)], w, gr)
-
-        def evacq(i, r):
-            c = ("Q", 512 * i, 512 * i + 512)
-            act(T.Q[:, c[1]:c[2]], T[r][:], [(r,)], [c], bias=1024.0 + 2 * i / 8192.0)
-
-        ring_evac(8, fillq, evacq)
-        pull(T.NX[:], ("NX",), "YFO", None)
-        tcopy(T.B16[:], T.SC[:, 15:256:16], [("SC",)], [("B16",)])
-        op("V", lambda: V.tensor_reduce(T.CNT[:, 0:1], T.MT[:], AxisListType.X, A_.add), [("MT",)], [("CNT", 0, 1)])
-        mm(T.SM[:, 16:17], T.BO[:], T.CNT[:, 0:1], True, True, [("BO",), ("CNT", 0, 1)], [("SM", 16, 17)], newgroup())
-        for j in range(2):
-            extract(128 * j, 128 * j + 128, j == 0)
-        ts(T.LP[:], T.KEY[:, 0:256], 2048.0, None, A_.add, None, [("KEY", 0, 256)], [("LP",)])
-        for j in range(4):
-            c = ("BIG", 1024 * j, 1024 * j + 1024)
-            ind = T.Q[:].indirect(T.LP[:, 64 * j:64 * j + 64])
-            if j % 2:
-                act(T.BIG[:, c[1]:c[2]], ind, [("Q",), ("LP",)], [c])
-            else:
-                tcopy(T.BIG[:, c[1]:c[2]], ind, [("Q",), ("LP",)], [c])
-        ts(T.JC[:], T.KEY[:, 0:256], 2048.0, None, A_.add, None, [("KEY", 0, 256)], [("JC",)])
-        tcopy(T.PJ[:, 0:1], T.SM[:, 16:17], [("SM", 16, 17)], [("PJ",)])
-        ts(T.PI[:, 0:1], T.PJ[:, 0:1], 31, None, A_.bitwise_and, None, [("PJ",)], [("PI",)])
-        ts(T.PC[:, 0:1], T.PI[:, 0:1], 16.0, None, A_.mult, None, [("PI",)], [("PC",)])
-        tt(T.THR[:, 0:1], T.PC[:, 0:1], T.TT[:, 0:1], A_.add, [("PC",), ("TT",)], [("THR",)])
+        for i in range(QA // 2):
+            if i >= 4:
+                qg.append(qfill(i))
+            qmark(i, qg[i])
+        vb = ["KEY", "HP", "SM"]
+        old = "Q" if t else "BIG"
+        for a in range(QA, 16):
+            r, e = vb[(a - QA) // 2 % 3], a % 2
+            w = (r, 256 * e, 256 * e + 256)
+            mm(T[r][:, 256 * e:256 * e + 256], T.BR[:, 128 * a:128 * a + 128], T.M16[:], True, True, [("BR",), ("M16",)], [w], newgroup())
+        for a in range(QA, 16):
+            r, e = vb[(a - QA) // 2 % 3], a % 2
+            tt(T.Q[:, a:4096:16], T[r][:, 256 * e:256 * e + 256], T[old][:, a:4096:16], A_.add, [(r, 256 * e, 256 * e + 256), ("Q%d" % a,) if t else ("BIG", 0, 4096)], [("Q%d" % a,)])
+        halves("JR", "Q", "LP", [("Q%d" % a,) for a in range(16)])
+        halves("BIG", "JR", "LP", [("JR",)])
         arrive("K%d" % (t + 1), "rk%d" % t)
         arrive("H%d" % (t + 1), "rh%d" % t)
 

@@ -5,7 +5,7 @@ A_ = AluOpType
 F = ActivationFunctionType
 CHUNKS = [(0, 64), (64, 128), (128, 192), (192, 256)]
 PICKS = [6, 1, 1, 1, 7]
-YV, YA = 3, 7
+YA = 6
 QA = 10
 BIAS = 262144.0
 NV = 4
@@ -20,10 +20,10 @@ SCRATCH = {
     "BIG": _sb(8448), "X": _sb(4096, "bfloat16"), "NX": _sb(4096, "int32"), "PL": _sb(4096, "int32"),
     "JR": _sb(4096), "Q": _sb(4096),
     "S": ("sbuf", [128, 256, 16], "float16"), "RL": ("sbuf", [128, 256, 16], "float16"),
-    "ERM": _sb(2048, "float16"), "EX": _sb(2048), "BR": _sb(2048, "bfloat16"), "IF": _sb(128), "SQ": _sb(256 * 4, "bfloat16"),
+    "ERM": _sb(2048, "float16"), "EX": _sb(2048), "BR": _sb(2048, "bfloat16"), "IF": _sb(128), "SQ": _sb(128 * 4, "bfloat16"), "IW": _sb(4096),
     "IB": _sb(128, "bfloat16"), "IH": _sb(128, "float16"), "BO": _sb(128), "BO8": _sb(8, "float16"),
-    "APA": _sb(128, "bfloat16"), "IOB": _sb(256, "bfloat16"), "OH": _sb(16), "DM": _sb(256), "RS": _sb(256), "RM": _sb(256),
-    "KC": _sb(256, "float16"), "CM": _sb(256, "float16"), "ZN": _sb(512, "float16"), "ZS": _sb(512, "float16"),
+    "APA": _sb(128, "bfloat16"), "IOB": _sb(128, "bfloat16"), "OH": _sb(16), "DM": _sb(256), "RS": _sb(256), "RM": _sb(256),
+    "KC": _sb(256, "bfloat16"), "CM": _sb(256, "float16"), "ZN": _sb(512, "float16"), "ZS": _sb(512, "float16"),
     "ZW": _sb(128, "float16"), "T0": _sb(512), "T1": _sb(512), "PI": _sb(2, "int32"),
     "PJ": _sb(2, "int32"), "FC": _sb(2), "GC": _sb(2), "PB": _sb(2), "PC": _sb(2),
     "NNI": _sb(256, "int32"), "NNF": _sb(256), "NNT": _sb(256), "SW": _sb(512),
@@ -39,10 +39,9 @@ SCRATCH = {
     "U1": _sb(16), "U2": _sb(16), "QF": _sb(16), "QXF": _sb(16), "QO": _sb(16, "uint16"), "QXO": _sb(16, "uint16"),
     "VI": _sb(16, "int32"), "FR": _sb(16), "YL": _sb(16), "YO": _sb(16, "uint16"), "VL": _sb(16), "VO": _sb(16, "uint16"), "NL": _sb(16),
     "GO": _sb(16), "W1": _sb(16), "W2": _sb(16), "YF": _sb(16), "YFO": _sb(16, "uint16"), "QNF": _sb(16), "QNO": _sb(16, "uint16"),
-    "WI": _sb(16, "int32"), "AB": _sb(32, "int32"), "ABY": _sb(32), "ABN": _sb(32), "Y16": _sb(16),
-    "RY": _sb(256 * (16 - YV), "bfloat16"), "LA": _sb(128 * NSLOT, "bfloat16"), "RB": _sb(256 * NSLOT, "bfloat16"),
+    "WI": _sb(16, "int32"), "AB": _sb(32, "int32"), "ABY": _sb(48), "ABN": _sb(48), "Y16": _sb(16),
+    "RY": _sb(128 * 16, "bfloat16"), "LA": _sb(128 * NSLOT, "bfloat16"), "RB": _sb(128 * NSLOT, "bfloat16"),
     "CNT": _sb(2), "M16": _sb(256, "bfloat16"), "C16": _sb(256, "bfloat16"), "DX": _sb(256), "JC": _sb(256),
-    "JL": _sb(256, "bfloat16"), "JH": _sb(256, "bfloat16"),
     "LP": _sb(256, "uint16"), "PSG": _sb(256), "ZZ": _sb(256),
     "YB": _sb(256), "YH": _sb(256, "bfloat16"),
     "R0": ("psum", [128, 512], "float32"), "R1": ("psum", [128, 512], "float32"),
@@ -181,6 +180,9 @@ def rank_program(g, core, T, topo):
     iota(T.T0[:, 128:256], [[0, 8], [1, 16]], 0, 0, [("T0", 128, 256)])
     iota(T.T0[0:8, 384:512], [[1, 8], [0, 16]], 0, -1, [("T0", 384, 512)])
     iota(T.B16[:], [[16, 16]], 0, 0, [("B16",)])
+    iota(T.KC[:], [[0, 16], [1, 16]], 0, 0, [("KC",)])
+    iota(T.IOB[:], [[1, 128]], 0, 0, [("IOB",)])
+    iota(T.IW[:], [[1, 4096]], 0, 0, [("IW",)])
     ts(T.PJ[:], T.PI[:], 15, None, A_.bitwise_and, None, [("PI",)], [("PJ",)])
     tcopy(T.FC[:], T.PJ[:], [("PJ",)], [("FC",)])
     ts(T.PI[:], T.PI[:], 4, None, A_.arith_shift_right, None, [("PI",)], [("PI",)])
@@ -199,11 +201,9 @@ def rank_program(g, core, T, topo):
     ts(T.ZN[:, 0:256], T.T1[:, 256:512], -256.0, None, A_.add, None, [col], [("ZN", 0, 256)])
     tcopy(T.ZN[:, 256:512], T.T1[:, 256:512], [col], [("ZN", 256, 512)])
     ts(T.CM[:], T.T1[:, 0:256], 0.0, -1026.0, A_.mult, A_.add, [("T1", 0, 256)], [("CM",)])
-    tcopy(T.KC[:], T.T1[:, 0:256], [("T1", 0, 256)], [("KC",)])
     ts(T.OH[:], T.T1[:, 256:272], fcol, None, A_.is_equal, None, [col, ("FC",)], [("OH",)])
     ts(T.BO[:], T.T0[:, 0:128], gcol, None, A_.is_equal, None, [("T0", 0, 128), ("GC",)], [("BO",)])
-    for k in range(16):
-        op("A", lambda: S_.activation(T.BR[:, 128 * k:128 * k + 128], T.BO[:], F.Identity, scale=T.OH[:, k:k + 1]), [("BO",), ("OH",)], [("BR", 128 * k, 128 * k + 128)])
+    ts(T.FR[:], T.OH[:], 768.0, None, A_.mult, None, [("OH",)], [("FR",)])
     ts(T.BO8[:], T.T1[:, 256:264], gcol, -16.0, A_.is_equal, A_.mult, [col, ("GC",)], [("BO8",)])
     for r in range(4):
         ts(T.ERM[:, 512 * r:512 * r + 512], T.ZN[:], 0.0, None, A_.mult, None, [("ZN",)], [("ERM", 512 * r, 512 * r + 512)])
@@ -212,7 +212,6 @@ def rank_program(g, core, T, topo):
         tcopy(T.ERM[:, 128 * r + r:128 * r + 128:16], T.BO8[:], [("BO8",), e], [e])
     ts(T.DM[:], T.T1[:, 0:256], fcol, None, A_.is_equal, None, [("T1", 0, 256), ("FC",)], [("DM",)])
     ts(T.RS[:], T.T1[:, 0:256], 0.0, None, A_.is_gt, None, [("T1", 0, 256)], [("RS",)])
-    ts(T.RM[:], T.RS[:], -2.0e9, 1.0e9, A_.mult, A_.add, [("RS",)], [("RM",)])
     ts(T.PS[0:8, 0:128], T.T0[0:8, 384:512], 0.0, None, A_.is_equal, None, [("T0", 384, 512)], [("PS",)])
     ts(T.LI[:], T.B16[:], fcol, None, A_.add, None, [("B16",), ("FC",)], [("LI",)])
     ts(T.HI[:], T.LI[:], 8192.0, None, A_.add, None, [("LI",)], [("HI",)])
@@ -226,10 +225,7 @@ def rank_program(g, core, T, topo):
         mm(T[r][:], T.IB[:], T.X[:, 512 * i:512 * i + 512], True, False, [("IB",), ("X", 512 * i, 512 * i + 512)], [(r,)], gr)
         mm(T[r][:], T.ZW[:], T.ZN[:], False, True, [("ZW",), ("ZN",)], [(r,)], gr)
         b = 1024.0 + (512 * i + 256 - 2048) / 8192.0
-        if i % 2:
-            act(T.BIG[:, c[1]:c[2]], T[r][:], [(r,)], [c], bias=b)
-        else:
-            ts(T.BIG[:, c[1]:c[2]], T[r][:], b, None, A_.add, None, [(r,)], [c])
+        act(T.BIG[:, c[1]:c[2]], T[r][:], [(r,)], [c], bias=b)
 
     def setup_late():
         tcopy(T.THF[0:8, :], T.THI[0:8, :], [("THI",)], [("THF",)])
@@ -244,7 +240,6 @@ def rank_program(g, core, T, topo):
         ts(T.APA[:], T.T0[:, 128:256], 1.0, None, A_.add, None, [("T0", 128, 256)], [("APA",)])
         tt(T.APA[:], T.APA[:], T.BO[:], A_.mult, [("APA",), ("BO",)], [("APA",)])
         ts(T.APA[:], T.APA[:], -1.0, None, A_.add, None, [("APA",)], [("APA",)])
-        ts(T.IOB[:], T.T1[:, 256:512], 1.0, None, A_.add, None, [col], [("IOB",)])
 
     def setup_last():
         tcopy(T.NNF[:], T.NNI[:], [("NNI",)], [("NNF",)])
@@ -269,41 +264,50 @@ def rank_program(g, core, T, topo):
     nslot = [0]
 
     def codes(src, gate, dst):
-        ts(T.Y16[:], T[src][:], 16.0, None, A_.add, None, [(src,)], [("Y16",)])
-        tt(T.WI[:], T.Y16[:], T[gate][:], A_.mult, [("Y16",), (gate,)], [("WI",)])
-        ts(T.AB[:, 0:16], T.WI[:], 15, None, A_.bitwise_and, None, [("WI",)], [("AB", 0, 16)])
-        ts(T.AB[:, 16:32], T.WI[:], 4, None, A_.arith_shift_right, None, [("WI",)], [("AB", 16, 32)])
-        tcopy(T[dst][:], T.AB[:], [("AB",)], [(dst,)])
+        return [
+            lambda: tcopy(T.WI[:], T[src][:], [(src,)], [("WI",)]),
+            lambda: ts(T.MKI[:], T.WI[:], 11, None, A_.arith_shift_right, None, [("WI",)], [("MKI",)]),
+            lambda: ts(T.AB[:, 0:16], T.WI[:], 15, None, A_.bitwise_and, None, [("WI",)], [("AB", 0, 16)]),
+            lambda: ts(T.AB[:, 16:32], T.WI[:], 4, 127, A_.arith_shift_right, A_.bitwise_and, [("WI",)], [("AB", 16, 32)]),
+            lambda: ts(T.Y16[:], T.MKI[:], 1023.0, 1.0, A_.mult, A_.add, [("MKI",)], [("Y16",)]),
+            lambda: tcopy(T[dst][:, 0:32], T.AB[:], [("AB",)], [(dst, 0, 32)]),
+            lambda: tt(T[dst][:, 32:48], T.Y16[:], T[gate][:], A_.mult, [("Y16",), (gate,)], [(dst, 32, 48)])]
+
+    def weave(*lists):
+        for n in range(max(len(x) for x in lists)):
+            for x in lists:
+                if n < len(x):
+                    x[n]()
 
     def scalar_codes(src, cols):
         for c in cols:
             s = c % 4
-            sq, rb = ("SQ", 256 * s, 256 * s + 256), ("RY", 256 * (c - YV), 256 * (c - YV) + 256)
+            sq = ("SQ", 128 * s, 128 * s + 128)
             op("A", lambda: S_.activation(T.SQ[:, sq[1]:sq[2]], T.IOB[:], F.Square, bias=T[src][:, 16 + c:17 + c], scale=-1.0), [("IOB",), (src,)], [sq])
             if c > cols[0]:
                 relu_codes(c - 1)
         relu_codes(cols[-1])
 
     def relu_codes(c):
-        sq, rb = ("SQ", 256 * (c % 4), 256 * (c % 4) + 256), ("RY", 256 * (c - YV), 256 * (c - YV) + 256)
+        sq, rb = ("SQ", 128 * (c % 4), 128 * (c % 4) + 128), ("RY", 128 * c, 128 * c + 128)
         op("A", lambda: S_.activation(T.RY[:, rb[1]:rb[2]], T.SQ[:, sq[1]:sq[2]], F.Relu, bias=1.0, scale=-1.0), [sq], [rb])
 
     def scalar_marks(src, cols, gr):
         for c in cols:
             s = nslot[0] % NSLOT
             nslot[0] += 1
-            la, rb = ("LA", 128 * s, 128 * s + 128), ("RY", 256 * (c - YV), 256 * (c - YV) + 256)
-            ts(T.LA[:, la[1]:la[2]], T.APA[:], T[src][:, c:c + 1], None, A_.is_equal, None, [("APA",), (src,)], [la])
-            mm(T.CN[:, 0:256], T.LA[:, la[1]:la[2]], T.RY[:, rb[1]:rb[2]], False, c == 15, [la, rb], [("CN", 0, 256)], gr)
+            la, rb = ("LA", 128 * s, 128 * s + 128), ("RY", 128 * c, 128 * c + 128)
+            ts(T.LA[:, la[1]:la[2]], T.APA[:], T[src][:, c:c + 1], T[src][:, 32 + c:33 + c], A_.is_equal, A_.mult, [("APA",), (src,)], [la])
+            mm(T.CN[:, 0:128], T.LA[:, la[1]:la[2]], T.RY[:, rb[1]:rb[2]], c == 0, c == 15, [la, rb], [("CN", 0, 128)], gr)
 
-    def marks(src, cols, first, last, gr):
+    def marks(src, cols, gr):
         for c in cols:
             s = nslot[0] % NSLOT
             nslot[0] += 1
-            la, rb = ("LA", 128 * s, 128 * s + 128), ("RB", 256 * s, 256 * s + 256)
-            ts(T.LA[:, la[1]:la[2]], T.APA[:], T[src][:, c:c + 1], None, A_.is_equal, None, [("APA",), (src,)], [la])
+            la, rb = ("LA", 128 * s, 128 * s + 128), ("RB", 128 * s, 128 * s + 128)
+            ts(T.LA[:, la[1]:la[2]], T.APA[:], T[src][:, c:c + 1], T[src][:, 32 + c:33 + c], A_.is_equal, A_.mult, [("APA",), (src,)], [la])
             ts(T.RB[:, rb[1]:rb[2]], T.IOB[:], T[src][:, 16 + c:17 + c], None, A_.is_equal, None, [("IOB",), (src,)], [rb])
-            mm(T.CN[:, 0:256], T.LA[:, la[1]:la[2]], T.RB[:, rb[1]:rb[2]], first and c == 0, last and c == 15, [la, rb], [("CN", 0, 256)], gr)
+            mm(T.CN[:, 0:128], T.LA[:, la[1]:la[2]], T.RB[:, rb[1]:rb[2]], False, False, [la, rb], [("CN", 0, 128)], gr)
 
     def to_hp(h):
         gr = newgroup()
@@ -316,9 +320,10 @@ def rank_program(g, core, T, topo):
         scan(T.SC[:], T.RS[:], T.Z[:], A_.mult, A_.add, [("RS",), ("Z",)], [("SC",)])
 
     def place(dst):
-        tcopy(T.VI[:], T.SC[:, 15:256:16], [("SC",)], [("VI",)])
-        tt(T.FR[:], T.SC[:, 15:256:16], T.VI[:], A_.subtract, [("SC",), ("VI",)], [("FR",)])
-        ts(T[dst][:], T.FR[:], 8192.0, 2048.0, A_.mult, A_.add, [("FR",)], [(dst,)])
+        return [
+            lambda: tcopy(T.VI[:], T.SC[:, 15:256:16], [("SC",)], [("VI",)]),
+            lambda: tt(T.FR[:], T.SC[:, 15:256:16], T.VI[:], A_.subtract, [("SC",), ("VI",)], [("FR",)]),
+            lambda: ts(T[dst][:], T.FR[:], 8192.0, 2048.0, A_.mult, A_.add, [("FR",)], [(dst,)])]
 
     def blend(out):
         tt(T.SS[:], T.F1[:], T.HP[:, 0:256], A_.add, [("F1",), ("HP", 0, 256)], [("SS",)])
@@ -332,10 +337,10 @@ def rank_program(g, core, T, topo):
                [("EX", 128 * k, 128 * k + 128), ("BIG", 0, 4096)], [("CN", 256, 512)], picked[1])
             picked[0] = k + 1
 
-    def halves(out, src, off, srcs):
-        for j in range(4):
-            c = (out, 1024 * j, 1024 * j + 1024)
-            ind = T[src][:, 0:4096].indirect(T[off][:, 64 * j:64 * j + 64])
+    def halves(out, src, off, srcs, n=2):
+        for j in range(n):
+            c = (out, 4096 // n * j, 4096 // n * (j + 1))
+            ind = T[src][:, 0:4096].indirect(T[off][:, 256 // n * j:256 // n * (j + 1)])
             if j % 2:
                 act(T[out][:, c[1]:c[2]], ind, srcs + [(off,)], [c])
             else:
@@ -387,6 +392,9 @@ def rank_program(g, core, T, topo):
             xc = ("BIG", 4096 + 16 * l0, 4096 + 16 * l1)
             act(T.BIG[:, xc[1]:xc[2]], T.BIG[:, 0:4096].indirect(T[kb][:, l0:l1]), [("BIG", 0, 4096), (kb,)], [xc])
         if t == 0:
+            op("A", lambda: S_.activation(T.RM[:], T.RS[:], F.Identity, bias=1.0e9, scale=-2.0e9), [("RS",)], [("RM",)])
+            for k in range(16):
+                op("A", lambda: S_.activation(T.BR[:, 128 * k:128 * k + 128], T.BO[:], F.Identity, scale=T.FR[:, k:k + 1]), [("BO",), ("FR",)], [("BR", 128 * k, 128 * k + 128)])
             setup_late()
         else:
             pull(T.NX[:], ("NX",), "YFO")
@@ -410,7 +418,7 @@ def rank_program(g, core, T, topo):
                    [("BIG", a, 4096 + 16 * l1), ("HP", 0, 256)], [s3], "s%d_%d" % (t, l0))
             ts(T.RL[:, l0:l1, :], T.S[:, l0:l1, :], -2.0, -2048.0, A_.mult, A_.min, [s3], [r3])
             picks(PICKS[n])
-            mm(T.KEY[:, l0:l1], T.IH[:], T.KC[:, l0:l1], True, False, [("IH",), ("KC",)], [ko], kgr)
+            mm(T.KEY[:, l0:l1], T.IB[:], T.KC[:, l0:l1], True, False, [("IB",), ("KC",)], [ko], kgr)
             for r in range(16):
                 mm(T.KEY[:, l0:l1], T.ERM[:, 128 * r:128 * r + 128], T.S[:, l0 + r:l1:16, :], False, False, [("ERM",), s3], [ko], kgr)
             for r in range(16):
@@ -431,9 +439,10 @@ def rank_program(g, core, T, topo):
         tcopy(T.QXO[:], T.QXF[:], [("QXF",)], [("QXO",)])
         act(T.F1[:], T.BIG[:].indirect(T.QXO[:]), [BW, ("QXO",)], [("F1",)])
         pull(T.BIG[:], BW, "QO")
-        place("YL")
-        tcopy(T.YO[:], T.YL[:], [("YL",)], [("YO",)])
-        pull(T.NX[:], ("NX",), "YO")
+        weave(place("YO"))
+        tt(T.Z[:], T.NX[:].indirect(T.YO[:]), T.DM[:], A_.mult, [("NX",), ("YO",), ("DM",)], [("Z",)])
+        ts(T.YL[:], T.FR[:], 8192.0, 2048.0, A_.mult, A_.add, [("FR",)], [("YL",)])
+        scan(T.SC[:], T.RS[:], T.Z[:], A_.mult, A_.add, [("RS",), ("Z",)], [("SC",)])
         tcopy(T.VO[:], T.SC[:, 15:256:16], [("SC",)], [("VO",)])
         tcopy(T.VL[:], T.SC[:, 15:256:16], [("SC",)], [("VL",)])
         blend("HA")
@@ -448,17 +457,16 @@ def rank_program(g, core, T, topo):
         for r in range(16):
             mm(T.SM[:, 0:16], T.ERM[:, 128 * r:128 * r + 128], T.R2[:, r:256:16], False, r == 15, [("ERM",), ("R2",)], [("SM", 0, 16)], g2)
         picks(16)
-        place("NL")
-        tt(T.W1[:], T.VL[:], T.HI[:], A_.subtract, [("VL",), ("HI",)], [("W1",)])
-        tt(T.W2[:], T.NL[:], T.YL[:], A_.subtract, [("NL",), ("YL",)], [("W2",)])
-        codes("YL", "MT", "ABY")
+        weave(place("NL") + [
+            lambda: tt(T.W2[:], T.NL[:], T.YL[:], A_.subtract, [("NL",), ("YL",)], [("W2",)]),
+            lambda: tt(T.W1[:], T.VL[:], T.HI[:], A_.subtract, [("VL",), ("HI",)], [("W1",)]),
+            lambda: tt(T.W2[:], T.W2[:], T.MT[:], A_.mult, [("W2",), ("MT",)], [("W2",)]),
+            lambda: tt(T.W1[:], T.W1[:], T.MT[:], A_.mult, [("W1",), ("MT",)], [("W1",)])], codes("YL", "MT", "ABY"))
         gm = newgroup()
-        scalar_codes("ABY", range(YV, YA))
+        scalar_codes("ABY", range(0, YA))
         if t:
-            tcopy(T.NNI[:], T.CN[:, 256:512], [("CN", 256, 512)], [("NNI",)])
             qg = [] if last else [qfill(i) for i in range(4)]
         ts(T.GO[:], T.SM[:, 0:16], T.TT[:, 1:2], None, A_.is_le, None, [("SM", 0, 16), ("TT",)], [("GO",)])
-        tt(T.GO[:], T.GO[:], T.MT[:], A_.mult, [("GO",), ("MT",)], [("GO",)])
         tt(T.W2[:], T.W2[:], T.GO[:], A_.mult, [("W2",), ("GO",)], [("W2",)])
         tt(T.W1[:], T.W1[:], T.GO[:], A_.mult, [("W1",), ("GO",)], [("W1",)])
         tt(T.YF[:], T.W2[:], T.YL[:], A_.add, [("W2",), ("YL",)], [("YF",)])
@@ -471,73 +479,63 @@ def rank_program(g, core, T, topo):
             tcopy(T[ks][:], T.PL[:].indirect(T.YFO[:]), [("PL",), ("YFO",)], [(ks,)])
             send("K%d" % (t + 1), ks, "rk%d" % t)
         scalar_codes("ABY", range(YA, 16))
-        if t:
-            tt(T.BMF[:], T.CN[:, 256:512], T.NNI[:], A_.subtract, [("CN", 256, 512), ("NNI",)], [("BMF",)])
-        codes("NL", "GO", "ABN")
-        marks("ABY", range(0, YV), True, False, gm)
         if t == 0:
             setup_last()
+        tt(T.U1[:], T.GO[:], T.MT[:], A_.mult, [("GO",), ("MT",)], [("U1",)])
+        lj = []
+        if t:
+            lj = [lambda: tcopy(T.NNI[:], T.CN[:, 256:512], [("CN", 256, 512)], [("NNI",)]), lambda: None,
+                  lambda: tt(T.BMF[:], T.CN[:, 256:512], T.NNI[:], A_.subtract, [("CN", 256, 512), ("NNI",)], [("BMF",)])]
+        weave(lj, codes("NL", "U1", "ABN"))
+        scalar_marks("ABY", range(0, YA), gm)
+        if t == 0:
             qg = [qfill(i) for i in range(4)]
             for k in range(16):
                 op("A", lambda: S_.activation(T.EX[:, 128 * k:128 * k + 128], T.IF[:], F.Identity, scale=T.OH[:, k:k + 1]), [("IF",), ("OH",)], [("EX", 128 * k, 128 * k + 128)])
         if not last:
             op("V", lambda: V.tensor_reduce(T.CNT[:, 0:1], T.MT[:], AxisListType.X, A_.add), [("MT",)], [("CNT", 0, 1)])
             mm(T.SM[:, 16:17], T.BO[:], T.CNT[:, 0:1], True, True, [("BO",), ("CNT", 0, 1)], [("SM", 16, 17)], newgroup())
-        marks("ABN", range(0, 6), False, False, gm)
+        if t == 0:
+            tt(T.DX[:], T.KEY[:, 0:256], T.PSG[:], A_.subtract, [("KEY", 0, 256), ("PSG",)], [("DX",)])
+        marks("ABN", range(0, 6), gm)
         blend(hs)
         if not last:
             send("H%d" % (t + 1), hs, "rh%d" % t)
-        marks("ABN", range(6, 16), False, False, gm)
+        marks("ABN", range(6, 16), gm)
         if t:
             ts(T.JC[:], T.BMF[:], 8192.0, 2048.0, A_.mult, A_.add, [("BMF",)], [("JC",)])
-        scalar_marks("ABY", range(YV, 16), gm)
         if not last:
             tcopy(T.PJ[:, 0:1], T.SM[:, 16:17], [("SM", 16, 17)], [("PJ",)])
-            ts(T.M16[:], T.CN[:, 0:256], 0.5, 768.0, A_.is_gt, A_.mult, [("CN", 0, 256)], [("M16",)])
-        if t == 0:
-            tt(T.DX[:], T.KEY[:, 0:256], T.PSG[:], A_.subtract, [("KEY", 0, 256), ("PSG",)], [("DX",)])
-        ts(T.ZZ[:], T.CN[:, 0:256], 0.5, None, A_.is_gt, None, [("CN", 0, 256)], [("ZZ",)])
-        tt(T.ZZ[:], T.ZZ[:], T.DX[:], A_.mult, [("ZZ",), ("DX",)], [("ZZ",)])
+        scalar_marks("ABY", range(YA, 16), gm)
+        tcopy(T.KI[:, 0:128], T.CN[:, 0:128], [("CN", 0, 128)], [("KI", 0, 128)])
+        ts(T.M16[:, 128:256], T.CN[:, 0:128], 1023.5, None, A_.is_gt, None, [("CN", 0, 128)], [("M16", 128, 256)])
+        ts(T.KI[:, 128:256], T.KI[:, 0:128], 1023, None, A_.bitwise_and, None, [("KI", 0, 128)], [("KI", 128, 256)])
+        ts(T.M16[:, 0:128], T.KI[:, 128:256], 0.5, None, A_.is_gt, None, [("KI", 128, 256)], [("M16", 0, 128)])
+        tt(T.ZZ[:], T.M16[:], T.DX[:], A_.mult, [("M16",), ("DX",)], [("ZZ",)])
         jold = "JC" if t else "PSG"
         tt(T.JC[:], T[jold][:], T.ZZ[:], A_.add, [(jold,), ("ZZ",)], [("JC",)])
-        if last:
-            tcopy(T.NNI[:], T.JC[:], [("JC",)], [("NNI",)])
-            ts(T.KI[:], T.NNI[:], 63, None, A_.bitwise_and, None, [("NNI",)], [("KI",)])
-            tcopy(T.JL[:], T.KI[:], [("KI",)], [("JL",)])
-            tt(T.JH[:], T.JC[:], T.KI[:], A_.subtract, [("JC",), ("KI",)], [("JH",)])
         tcopy(T.LP[:], T.JC[:], [("JC",)], [("LP",)])
         if last:
-            for i in range(8):
-                r = RING[i % 4]
-                for e in range(2):
-                    a = 2 * i + e
-                    for n, j in enumerate(("JL", "JH")):
-                        mm(T[r][:, 256 * e:256 * e + 256], T.BR[:, 128 * a:128 * a + 128], T[j][:], n == 0, n == 1, [("BR",), (j,)], [(r, 256 * e, 256 * e + 256)], ("j", i))
-                for e in range(2):
-                    a = 2 * i + e
-                    if i % 2:
-                        op("A", lambda: S_.activation(T.JR[:, a:4096:16], T[r][:, 256 * e:256 * e + 256], F.Copy), [(r,)], [("JR",)], "jr")
-                    else:
-                        op("V", lambda: V.tensor_copy(T.JR[:, a:4096:16], T[r][:, 256 * e:256 * e + 256]), [(r,)], [("JR",)], "jr")
-            halves("Q", "JR", "LP", [("JR",)])
+            halves("JR", "IW", "LP", [("IW",)])
             tcopy(T.YB[:], T.NX[:].indirect(T.YFO[:]), [("NX",), ("YFO",)], [("YB",)])
             ts(T.YH[:], T[hs][:], -1026.0, None, A_.add, None, [(hs,)], [("YH",)])
             dma("S", T.yb[:], T.YB[0:128:16, :], [("YB",)], [])
             dma("S", T.yh[:], T.YH[:], [("YH",)], [])
+            halves("Q", "JR", "LP", [("JR",)], 4)
             for j in range(4):
                 c = (1024 * j, 1024 * j + 1024)
                 dma("S", T.yj[:, c[0]:c[1]], T.Q[0:128:16, c[0]:c[1]], [("Q",) + c], [])
             break
+        vb = ["KEY", "HP", "SM"]
+        old = "Q" if t else "BIG"
         for i in range(QA // 2):
             if i >= 4:
                 qg.append(qfill(i))
             qmark(i, qg[i])
-        vb = ["KEY", "HP", "SM"]
-        old = "Q" if t else "BIG"
-        for a in range(QA, 16):
-            r, e = vb[(a - QA) // 2 % 3], a % 2
-            w = (r, 256 * e, 256 * e + 256)
-            mm(T[r][:, 256 * e:256 * e + 256], T.BR[:, 128 * a:128 * a + 128], T.M16[:], True, True, [("BR",), ("M16",)], [w], newgroup())
+            for a in range(QA + 2 * i, min(QA + 2 * i + 2, 16)):
+                r, e = vb[i], a % 2
+                w = (r, 256 * e, 256 * e + 256)
+                mm(T[r][:, 256 * e:256 * e + 256], T.BR[:, 128 * a:128 * a + 128], T.M16[:], True, True, [("BR",), ("M16",)], [w], newgroup())
         for a in range(QA, 16):
             r, e = vb[(a - QA) // 2 % 3], a % 2
             tt(T.Q[:, a:4096:16], T[r][:, 256 * e:256 * e + 256], T[old][:, a:4096:16], A_.add, [(r, 256 * e, 256 * e + 256), ("Q%d" % a,) if t else ("BIG", 0, 4096)], [("Q%d" % a,)])

from concourse.bass import DstId, RemoteDMATransfer
from concourse.mybir import dt, AluOpType, AxisListType, ActivationFunctionType

A_ = AluOpType
F = ActivationFunctionType
CHUNKS = [(0, 64), (64, 128), (128, 192), (192, 256)]
PICKS = [6, 1, 1, 1, 7]
YA = 6
QA = 10
BIAS = 262144.0
NV = 4
NSLOT = 8


def _sb(n, d="float32", p=128):
    return ("sbuf", [p, n], d)


SCRATCH = {
    "BIG": _sb(8448), "X": _sb(4096, "bfloat16"), "NX": _sb(4096, "int32"), "PL": _sb(4096, "int32"),
    "JR": _sb(4096), "Q": _sb(4096),
    "S": ("sbuf", [128, 256, 16], "float16"), "RL": ("sbuf", [128, 256, 16], "float16"),
    "ERM": _sb(2048, "float16"), "EX": _sb(2048), "BR": _sb(2048, "bfloat16"), "IF": _sb(128), "SQ": _sb(128 * 4, "bfloat16"), "IW": _sb(4096),
    "IB": _sb(128, "bfloat16"), "IH": _sb(128, "float16"), "BO": _sb(128), "BO8": _sb(8, "float16"),
    "APA": _sb(128, "bfloat16"), "IOB": _sb(128, "bfloat16"), "OH": _sb(16), "DM": _sb(256), "RS": _sb(256), "RM": _sb(256),
    "KC": _sb(256, "bfloat16"), "CM": _sb(256, "float16"), "ZN": _sb(512, "float16"), "ZS": _sb(512, "float16"),
    "ZW": _sb(128, "float16"), "T0": _sb(512), "T1": _sb(512), "PI": _sb(2, "int32"),
    "PJ": _sb(2, "int32"), "FC": _sb(2), "GC": _sb(2), "PB": _sb(2), "PC": _sb(2),
    "NNI": _sb(256, "int32"), "NNF": _sb(256), "NNT": _sb(256), "SW": _sb(512),
    "KI": _sb(256, "int32"), "HB": _sb(256, "bfloat16"), "THI": _sb(2, "int32"), "THF": _sb(2), "BMI": _sb(256, "int32"),
    "BMF": _sb(256), "TT": _sb(2), "THR": _sb(2),
    "K0": _sb(256, "uint16"), "K1": _sb(256, "uint16"), "K2": _sb(256, "uint16"), "K3": _sb(256, "uint16"),
    "H0": _sb(256, "float16"), "H1": _sb(256, "float16"), "H2": _sb(256, "float16"), "H3": _sb(256, "float16"),
    "KS0": _sb(256, "uint16"), "KS1": _sb(256, "uint16"), "KS2": _sb(256, "uint16"),
    "HS0": _sb(256, "float16"), "HS1": _sb(256, "float16"), "HS2": _sb(256, "float16"), "HS3": _sb(256, "float16"),
    "HA": _sb(256, "float16"),
    "PS": _sb(256), "SC": _sb(256), "Z": _sb(256), "F1": _sb(256), "SS": _sb(256), "S2": _sb(256, "float16"), "R2": _sb(256, "float16"),
    "MT": _sb(16), "MKI": _sb(16, "int32"), "KWI": _sb(16, "int32"), "LI": _sb(16), "E0": _sb(16), "E1": _sb(16), "E2": _sb(16), "HI": _sb(16), "B16": _sb(16),
    "U1": _sb(16), "U2": _sb(16), "QF": _sb(16), "QXF": _sb(16), "QO": _sb(16, "uint16"), "QXO": _sb(16, "uint16"),
    "VI": _sb(16, "int32"), "FR": _sb(16), "YL": _sb(16), "YO": _sb(16, "uint16"), "VL": _sb(16), "VO": _sb(16, "uint16"), "NL": _sb(16),
    "GO": _sb(16), "W1": _sb(16), "W2": _sb(16), "YF": _sb(16), "YFO": _sb(16, "uint16"), "QNF": _sb(16), "QNO": _sb(16, "uint16"),
    "WI": _sb(16, "int32"), "AB": _sb(32, "int32"), "ABY": _sb(48), "ABN": _sb(48), "Y16": _sb(16),
    "RY": _sb(128 * 16, "bfloat16"), "LA": _sb(128 * NSLOT, "bfloat16"), "RB": _sb(128 * NSLOT, "bfloat16"),
    "CNT": _sb(2), "M16": _sb(256, "bfloat16"), "C16": _sb(256, "bfloat16"), "DX": _sb(256), "JC": _sb(256),
    "LP": _sb(256, "uint16"), "PSG": _sb(256), "ZZ": _sb(256),
    "YB": _sb(256), "YH": _sb(256, "bfloat16"),
    "R0": ("psum", [128, 512], "float32"), "R1": ("psum", [128, 512], "float32"),
    "R2P": ("psum", [128, 512], "float32"), "R3": ("psum", [128, 512], "float32"),
    "KEY": ("psum", [128, 512], "float32"), "HP": ("psum", [128, 512], "float32"),
    "CN": ("psum", [128, 512], "float32"), "SM": ("psum", [128, 512], "float32"),
}
RING = ["R0", "R1", "R2P", "R3"]
PSUM = RING + ["KEY", "HP", "CN", "SM"]
NDMA = 40
SEMAPHORES = ["cV", "cA", "cT", "cG"] + ["d%d" % i for i in range(NDMA)] + ["rh%d" % t for t in range(3)] + ["rk%d" % t for t in range(3)] + ["ls"]


def rank_program(g, core, T, topo):
    rank = T.rank_of(core)
    if rank is None:
        return
    queue = {"V": g.vector, "A": g.scalar, "T": g.tensor, "G": g, "S": g.sync}
    count = {"V": 0, "A": 0, "T": 0, "G": 0}
    known = {"V": {}, "A": {}, "T": {}, "G": {}, "S": {}}
    snap = {}
    acc = {}
    ndma = [0]

    def need(q, sem, val):
        k = known[q]
        if k.get(sem, 0) >= val:
            return
        queue[q].wait_ge(T.sem[sem], val)
        k[sem] = val
        for s, v in snap.get((sem, val), {}).items():
            if k.get(s, 0) < v:
                k[s] = v

    def span(a):
        return a if len(a) == 3 else (a[0], 0, 1 << 30)

    def deps(q, reads, writes, group):
        w = {}
        for lst, wr in ((reads, False), (writes, True)):
            for a in lst:
                b, lo, hi = span(a)
                for (l, h, ow, oq, s, v, gr) in acc.get(b, []):
                    if b in PSUM and oq != q:
                        pass
                    elif not (lo < h and l < hi) or not (wr or ow):
                        continue
                    elif group is not None and gr == group:
                        continue
                    if w.get(s, 0) < v:
                        w[s] = v
        for s, v in sorted(w.items(), key=lambda e: -len(snap.get(e, {}))):
            need(q, s, v)

    def note(q, reads, writes, sem, val, group):
        snap[(sem, val)] = dict(known[q]) if q in known else {}
        for lst, wr in ((reads, False), (writes, True)):
            for a in lst:
                b, lo, hi = span(a)
                old = acc.get(b, [])
                if wr:
                    old = [e for e in old if not (lo <= e[0] and e[1] <= hi and known.get(q, {}).get(e[4], 0) >= e[5])]
                else:
                    old = [e for e in old if not (not e[2] and e[3] == q and lo <= e[0] and e[1] <= hi and e[4] == sem)]
                old.append((lo, hi, wr, q, sem, val, group))
                acc[b] = old

    def op(q, fn, reads, writes, group=None):
        deps(q, reads, writes, group)
        count[q] += 1
        fn().then_inc(T.sem["c" + q], 1)
        note(q, reads, writes, "c" + q, count[q], group)

    def dma(q, out, in_, reads, writes):
        deps(q, reads, writes, None)
        name = "d%d" % ndma[0]
        ndma[0] += 1
        queue[q].dma_start(out, in_).then_inc(T.sem[name], 16)
        note("dma", reads, writes, name, 16, None)
        snap[(name, 16)] = dict(known[q])

    def dmas(q, pairs, writes):
        name = "d%d" % ndma[0]
        ndma[0] += 1
        for o, i in pairs:
            queue[q].dma_start(o, i).then_inc(T.sem[name], 16)
        note("dma", [], writes, name, 16 * len(pairs), None)

    V, S_, TE = g.vector, g.scalar, g.tensor

    def tcopy(out, in_, r, w):
        op("V", lambda: V.tensor_copy(out, in_), r, w)

    def tt(out, a, b, o, r, w, group=None):
        op("V", lambda: V.tensor_tensor(out, a, b, o), r, w, group)

    def ts(out, a, s1, s2, o0, o1, r, w):
        if o1 is None:
            op("V", lambda: V.tensor_scalar(out, a, s1, s2, o0), r, w)
        else:
            op("V", lambda: V.tensor_scalar(out, a, s1, s2, o0, o1), r, w)

    def act(out, in_, r, w, bias=0.0):
        op("A", lambda: S_.activation(out, in_, F.Identity, bias=bias), r, w)

    def scan(out, d0, d1, o0, o1, r, w):
        op("V", lambda: V.tensor_tensor_scan(out, d0, d1, 0.0, o0, o1), r, w)

    def mm(out, l, rh, st, sp, r, w, group):
        op("T", lambda: TE.matmul(out, l, rh, st, sp), r, w, group)

    def iota(out, pat, base, cm, w):
        op("G", lambda: g.iota(out, pat, base, cm, allow_small_or_imprecise_dtypes=True), [], w)

    gid = [0]

    def newgroup():
        gid[0] += 1
        return gid[0]

    dma("S", T.KI[:], T.kt[:], [], [("KI",)])
    dma("S", T.HB[:], T.hm[:], [], [("HB",)])
    dma("A", T.NNI[:], T.nx[:], [], [("NNI",)])
    dma("A", T.THI[0:8, :], T.th[:], [], [("THI",)])
    dma("A", T.BMI[0:8, :], T.bm[:], [], [("BMI",)])
    for j in range(4):
        dma("S", T.X[:, 1024 * j:1024 * j + 1024], T.xp[:, 1024 * j:1024 * j + 1024], [], [("X", 1024 * j, 1024 * j + 1024)])
    dmas("S", [(T.NX[k:128:16, :], T.nx[:]) for k in range(16)], [("NX",)])
    dma("S", T.PL[:], T.pl[:], [], [("PL",)])

    op("G", lambda: g.iota(T.PI[:], [[0, 2]], 0, 1), [], [("PI",)])
    iota(T.T0[:, 256:384], [[1, 128]], 0, -1, [("T0", 256, 384)])
    iota(T.T1[:, 256:512], [[1, 256]], 0, 0, [("T1", 256, 512)])
    iota(T.T0[:, 0:128], [[1, 8], [0, 16]], 0, 0, [("T0", 0, 128)])
    iota(T.T1[:, 0:256], [[0, 16], [1, 16]], 0, 0, [("T1", 0, 256)])
    iota(T.T0[:, 128:256], [[0, 8], [1, 16]], 0, 0, [("T0", 128, 256)])
    iota(T.T0[0:8, 384:512], [[1, 8], [0, 16]], 0, -1, [("T0", 384, 512)])
    iota(T.B16[:], [[16, 16]], 0, 0, [("B16",)])
    iota(T.KC[:], [[0, 16], [1, 16]], 0, 0, [("KC",)])
    iota(T.IOB[:], [[1, 128]], 0, 0, [("IOB",)])
    iota(T.IW[:], [[1, 4096]], 0, 0, [("IW",)])
    ts(T.PJ[:], T.PI[:], 15, None, A_.bitwise_and, None, [("PI",)], [("PJ",)])
    tcopy(T.FC[:], T.PJ[:], [("PJ",)], [("FC",)])
    ts(T.PI[:], T.PI[:], 4, None, A_.arith_shift_right, None, [("PI",)], [("PI",)])
    tcopy(T.GC[:], T.PI[:], [("PI",)], [("GC",)])
    ts(T.PJ[:], T.PI[:], 1, None, A_.bitwise_and, None, [("PI",)], [("PJ",)])
    tcopy(T.PB[:, 1:2], T.PJ[:, 1:2], [("PJ",)], [("PB", 1, 2)])
    ts(T.PB[:, 0:1], T.PJ[:, 0:1], -1.0, 1.0, A_.mult, A_.add, [("PJ",)], [("PB", 0, 1)])
    fcol, gcol = T.FC[:, 0:1], T.GC[:, 0:1]
    tcopy(T.K0[:], T.KI[:], [("KI",)], [("K0",)])
    ts(T.H0[:], T.HB[:], 1026.0, None, A_.add, None, [("HB",)], [("H0",)])
    mp = ("T0", 256, 384)
    ts(T.IB[:], T.T0[:, 256:384], 0.0, None, A_.is_equal, None, [mp], [("IB",)])
    ts(T.IH[:], T.T0[:, 256:384], 0.0, None, A_.is_equal, None, [mp], [("IH",)])
    ts(T.ZW[:], T.T0[:, 256:384], 0.0, 1.0 / 8192, A_.is_equal, A_.mult, [mp], [("ZW",)])
    col = ("T1", 256, 512)
    ts(T.ZN[:, 0:256], T.T1[:, 256:512], -256.0, None, A_.add, None, [col], [("ZN", 0, 256)])
    tcopy(T.ZN[:, 256:512], T.T1[:, 256:512], [col], [("ZN", 256, 512)])
    ts(T.CM[:], T.T1[:, 0:256], 0.0, -1026.0, A_.mult, A_.add, [("T1", 0, 256)], [("CM",)])
    ts(T.OH[:], T.T1[:, 256:272], fcol, None, A_.is_equal, None, [col, ("FC",)], [("OH",)])
    ts(T.BO[:], T.T0[:, 0:128], gcol, None, A_.is_equal, None, [("T0", 0, 128), ("GC",)], [("BO",)])
    ts(T.FR[:], T.OH[:], 768.0, None, A_.mult, None, [("OH",)], [("FR",)])
    ts(T.BO8[:], T.T1[:, 256:264], gcol, -16.0, A_.is_equal, A_.mult, [col, ("GC",)], [("BO8",)])
    for r in range(4):
        ts(T.ERM[:, 512 * r:512 * r + 512], T.ZN[:], 0.0, None, A_.mult, None, [("ZN",)], [("ERM", 512 * r, 512 * r + 512)])
    for r in range(16):
        e = ("ERM", 128 * r, 128 * r + 128)
        tcopy(T.ERM[:, 128 * r + r:128 * r + 128:16], T.BO8[:], [("BO8",), e], [e])
    ts(T.DM[:], T.T1[:, 0:256], fcol, None, A_.is_equal, None, [("T1", 0, 256), ("FC",)], [("DM",)])
    ts(T.RS[:], T.T1[:, 0:256], 0.0, None, A_.is_gt, None, [("T1", 0, 256)], [("RS",)])
    ts(T.PS[0:8, 0:128], T.T0[0:8, 384:512], 0.0, None, A_.is_equal, None, [("T0", 384, 512)], [("PS",)])
    ts(T.LI[:], T.B16[:], fcol, None, A_.add, None, [("B16",), ("FC",)], [("LI",)])
    ts(T.HI[:], T.LI[:], 8192.0, None, A_.add, None, [("LI",)], [("HI",)])
    ts(T.E2[:], T.LI[:], 15.0, -4096.0, A_.mult, A_.add, [("LI",)], [("E2",)])
    tt(T.E0[:], T.HI[:], T.E2[:], A_.add, [("HI",), ("E2",)], [("E0",)])

    for i in range(8):
        r = RING[i % 4]
        gr = newgroup()
        c = ("BIG", 512 * i, 512 * i + 512)
        mm(T[r][:], T.IB[:], T.X[:, 512 * i:512 * i + 512], True, False, [("IB",), ("X", 512 * i, 512 * i + 512)], [(r,)], gr)
        mm(T[r][:], T.ZW[:], T.ZN[:], False, True, [("ZW",), ("ZN",)], [(r,)], gr)
        b = 1024.0 + (512 * i + 256 - 2048) / 8192.0
        act(T.BIG[:, c[1]:c[2]], T[r][:], [(r,)], [c], bias=b)

    def setup_late():
        tcopy(T.THF[0:8, :], T.THI[0:8, :], [("THI",)], [("THF",)])
        tcopy(T.BMF[0:8, :], T.BMI[0:8, :], [("BMI",)], [("BMF",)])
        mm(T.SM[:, 0:2], T.PS[0:8, 0:128], T.THF[0:8, :], True, True, [("PS",), ("THF",)], [("SM", 0, 2)], newgroup())
        mm(T.SM[:, 256:512], T.PS[0:8, 0:128], T.BMF[0:8, :], True, True, [("PS",), ("BMF",)], [("SM", 256, 512)], newgroup())
        ts(T.TT[:], T.SM[:, 0:2], 16.0, BIAS, A_.mult, A_.add, [("SM", 0, 2)], [("TT",)])
        tcopy(T.THR[:], T.TT[:], [("TT",)], [("THR",)])
        tt(T.Z[:], T.SM[:, 256:512], T.DM[:], A_.mult, [("SM", 256, 512), ("DM",)], [("Z",)])
        scan(T.SC[:], T.RS[:], T.Z[:], A_.mult, A_.add, [("RS",), ("Z",)], [("SC",)])
        tcopy(T.B16[:], T.SC[:, 15:256:16], [("SC",)], [("B16",)])
        ts(T.APA[:], T.T0[:, 128:256], 1.0, None, A_.add, None, [("T0", 128, 256)], [("APA",)])
        tt(T.APA[:], T.APA[:], T.BO[:], A_.mult, [("APA",), ("BO",)], [("APA",)])
        ts(T.APA[:], T.APA[:], -1.0, None, A_.add, None, [("APA",)], [("APA",)])

    def setup_last():
        tcopy(T.NNF[:], T.NNI[:], [("NNI",)], [("NNF",)])
        op("V", lambda: V.transpose(T.NNT[:], T.NNF[:]), [("NNF",)], [("NNT",)])
        for be in range(2):
            for ga in range(2):
                w = 128 * (2 * be + ga)
                ts(T.SW[:, w:w + 128], T.T0[:, 256:384], float(16 * (ga - be)), T.PB[:, be:be + 1], A_.is_equal, A_.mult, [mp, ("PB",)], [("SW", w, w + 128)])
        gr = newgroup()
        for be in range(2):
            for b in range(8):
                for ga in range(2):
                    w = 128 * (2 * be + ga)
                    mm(T.KEY[:, 2 * b + be:256:16], T.SW[:, w:w + 128], T.NNT[:, 32 * b + 16 * ga:32 * b + 16 * ga + 16], ga == 0, ga == 1,
                       [("SW", w, w + 128), ("NNT",)], [("KEY", 0, 256)], gr)
        ts(T.PSG[:], T.T1[:, 256:512], 16.0, fcol, A_.mult, A_.add, [col, ("FC",)], [("PSG",)])
        ts(T.IF[:], T.T0[:, 256:384], 0.0, None, A_.is_equal, None, [mp], [("IF",)])
        ts(T.ZS[:, 0:256], T.T1[:, 256:512], 16.0, -2048.0, A_.mult, A_.add, [col], [("ZS", 0, 256)])
        ts(T.ZS[:, 256:512], T.T1[:, 256:512], 16.0, -2047.0, A_.mult, A_.add, [col], [("ZS", 256, 512)])

    BW = ("BIG", 0, 8448)
    nslot = [0]

    def codes(src, gate, dst):
        return [
            lambda: tcopy(T.WI[:], T[src][:], [(src,)], [("WI",)]),
            lambda: ts(T.MKI[:], T.WI[:], 11, None, A_.arith_shift_right, None, [("WI",)], [("MKI",)]),
            lambda: ts(T.AB[:, 0:16], T.WI[:], 15, None, A_.bitwise_and, None, [("WI",)], [("AB", 0, 16)]),
            lambda: ts(T.AB[:, 16:32], T.WI[:], 4, 127, A_.arith_shift_right, A_.bitwise_and, [("WI",)], [("AB", 16, 32)]),
            lambda: ts(T.Y16[:], T.MKI[:], 1023.0, 1.0, A_.mult, A_.add, [("MKI",)], [("Y16",)]),
            lambda: tcopy(T[dst][:, 0:32], T.AB[:], [("AB",)], [(dst, 0, 32)]),
            lambda: tt(T[dst][:, 32:48], T.Y16[:], T[gate][:], A_.mult, [("Y16",), (gate,)], [(dst, 32, 48)])]

    def weave(*lists):
        for n in range(max(len(x) for x in lists)):
            for x in lists:
                if n < len(x):
                    x[n]()

    def scalar_codes(src, cols):
        for c in cols:
            s = c % 4
            sq = ("SQ", 128 * s, 128 * s + 128)
            op("A", lambda: S_.activation(T.SQ[:, sq[1]:sq[2]], T.IOB[:], F.Square, bias=T[src][:, 16 + c:17 + c], scale=-1.0), [("IOB",), (src,)], [sq])
            if c > cols[0]:
                relu_codes(c - 1)
        relu_codes(cols[-1])

    def relu_codes(c):
        sq, rb = ("SQ", 128 * (c % 4), 128 * (c % 4) + 128), ("RY", 128 * c, 128 * c + 128)
        op("A", lambda: S_.activation(T.RY[:, rb[1]:rb[2]], T.SQ[:, sq[1]:sq[2]], F.Relu, bias=1.0, scale=-1.0), [sq], [rb])

    def scalar_marks(src, cols, gr):
        for c in cols:
            s = nslot[0] % NSLOT
            nslot[0] += 1
            la, rb = ("LA", 128 * s, 128 * s + 128), ("RY", 128 * c, 128 * c + 128)
            ts(T.LA[:, la[1]:la[2]], T.APA[:], T[src][:, c:c + 1], T[src][:, 32 + c:33 + c], A_.is_equal, A_.mult, [("APA",), (src,)], [la])
            mm(T.CN[:, 0:128], T.LA[:, la[1]:la[2]], T.RY[:, rb[1]:rb[2]], c == 0, c == 15, [la, rb], [("CN", 0, 128)], gr)

    def marks(src, cols, gr):
        for c in cols:
            s = nslot[0] % NSLOT
            nslot[0] += 1
            la, rb = ("LA", 128 * s, 128 * s + 128), ("RB", 128 * s, 128 * s + 128)
            ts(T.LA[:, la[1]:la[2]], T.APA[:], T[src][:, c:c + 1], T[src][:, 32 + c:33 + c], A_.is_equal, A_.mult, [("APA",), (src,)], [la])
            ts(T.RB[:, rb[1]:rb[2]], T.IOB[:], T[src][:, 16 + c:17 + c], None, A_.is_equal, None, [("IOB",), (src,)], [rb])
            mm(T.CN[:, 0:128], T.LA[:, la[1]:la[2]], T.RB[:, rb[1]:rb[2]], False, False, [la, rb], [("CN", 0, 128)], gr)

    def to_hp(h):
        gr = newgroup()
        mm(T.HP[:, 0:256], T.IH[:], T[h][:], True, False, [("IH",), (h,)], [("HP", 0, 256)], gr)
        mm(T.HP[:, 0:256], T.IH[:], T.CM[:], False, True, [("IH",), ("CM",)], [("HP", 0, 256)], gr)
        act(T.BIG[:, 8192:8448], T.HP[:, 0:256], [("HP", 0, 256)], [("BIG", 8192, 8448)], bias=1024.0)

    def pull(win, wr, off):
        tt(T.Z[:], win.indirect(T[off][:]), T.DM[:], A_.mult, [wr, (off,), ("DM",)], [("Z",)])
        scan(T.SC[:], T.RS[:], T.Z[:], A_.mult, A_.add, [("RS",), ("Z",)], [("SC",)])

    def place(dst):
        return [
            lambda: tcopy(T.VI[:], T.SC[:, 15:256:16], [("SC",)], [("VI",)]),
            lambda: tt(T.FR[:], T.SC[:, 15:256:16], T.VI[:], A_.subtract, [("SC",), ("VI",)], [("FR",)]),
            lambda: ts(T[dst][:], T.FR[:], 8192.0, 2048.0, A_.mult, A_.add, [("FR",)], [(dst,)])]

    def blend(out):
        tt(T.SS[:], T.F1[:], T.HP[:, 0:256], A_.add, [("F1",), ("HP", 0, 256)], [("SS",)])
        ts(T[out][:], T.SS[:], 0.5, 513.75, A_.mult, A_.add, [("SS",)], [(out,)])

    picked = [16, 0]

    def picks(n):
        for k in range(picked[0], min(16, picked[0] + n)):
            mm(T.CN[:, 256:512], T.EX[:, 128 * k:128 * k + 128], T.BIG[:, k:4096:16], k == 0, k == 15,
               [("EX", 128 * k, 128 * k + 128), ("BIG", 0, 4096)], [("CN", 256, 512)], picked[1])
            picked[0] = k + 1

    def halves(out, src, off, srcs, n=2):
        for j in range(n):
            c = (out, 4096 // n * j, 4096 // n * (j + 1))
            ind = T[src][:, 0:4096].indirect(T[off][:, 256 // n * j:256 // n * (j + 1)])
            if j % 2:
                act(T[out][:, c[1]:c[2]], ind, srcs + [(off,)], [c])
            else:
                tcopy(T[out][:, c[1]:c[2]], ind, srcs + [(off,)], [c])

    nxt = T.cores[(rank + 1) % len(T.cores)]
    mask = topo.mask(core, nxt)
    rid, pid, _s = topo.addr(nxt)
    prv = T.cores[(rank - 1) % len(T.cores)]
    neng = len(topo.engines(core, nxt))
    nprv = len(topo.engines(prv, core))
    sent = [0]

    def send(dst, src, sem):
        deps("G", [(src,)], [], None)
        g.remote_dma(T[dst][:], T[src][:], T.sem[sem], T.sem.ls, pid, rid, mask)
        sent[0] += neng

    def arrive(dst, sem):
        note("remote", [], [(dst,)], sem, nprv, None)

    def qfill(i):
        r = RING[i % 4]
        gr = newgroup()
        mm(T[r][:], T.ZW[:], T.ZS[:], True, False, [("ZW",), ("ZS",)], [(r,)], gr)
        for e in range(2):
            a = 2 * i + e
            mm(T[r][:, 256 * e:256 * e + 256], T.IB[:], T.X[:, a:4096:16], False, False, [("IB",), ("X",)], [(r,)], gr)
            if t:
                mm(T[r][:, 256 * e:256 * e + 256], T.BR[:, 128 * a:128 * a + 128], T.C16[:], False, False, [("BR",), ("C16",)], [(r,)], gr)
        return gr

    def qmark(i, gr):
        r = RING[i % 4]
        for e in range(2):
            a = 2 * i + e
            mm(T[r][:, 256 * e:256 * e + 256], T.BR[:, 128 * a:128 * a + 128], T.M16[:], False, e == 1, [("BR",), ("M16",)], [(r,)], gr)
        for e in range(2):
            a = 2 * i + e
            act(T.Q[:, a:4096:16], T[r][:, 256 * e:256 * e + 256], [(r,)], [("Q%d" % a,)], bias=1024.0 + 2 * i / 8192.0)

    for t in range(NV):
        last = t == NV - 1
        kb, hb, hs = "K%d" % t, "H%d" % t, "HS%d" % t
        if t:
            picked[0], picked[1] = 0, newgroup()
        to_hp(hb)
        for (l0, l1) in CHUNKS:
            xc = ("BIG", 4096 + 16 * l0, 4096 + 16 * l1)
            act(T.BIG[:, xc[1]:xc[2]], T.BIG[:, 0:4096].indirect(T[kb][:, l0:l1]), [("BIG", 0, 4096), (kb,)], [xc])
        if t == 0:
            op("A", lambda: S_.activation(T.RM[:], T.RS[:], F.Identity, bias=1.0e9, scale=-2.0e9), [("RS",)], [("RM",)])
            for k in range(16):
                op("A", lambda: S_.activation(T.BR[:, 128 * k:128 * k + 128], T.BO[:], F.Identity, scale=T.FR[:, k:k + 1]), [("BO",), ("FR",)], [("BR", 128 * k, 128 * k + 128)])
            setup_late()
        else:
            pull(T.NX[:], ("NX",), "YFO")
            tcopy(T.B16[:], T.SC[:, 15:256:16], [("SC",)], [("B16",)])
            ts(T.PI[:, 0:1], T.PJ[:, 0:1], 31, None, A_.bitwise_and, None, [("PJ",)], [("PI",)])
            ts(T.PC[:, 0:1], T.PI[:, 0:1], 16.0, None, A_.mult, None, [("PI",)], [("PC",)])
            tt(T.THR[:, 0:1], T.PC[:, 0:1], T.TT[:, 0:1], A_.add, [("PC",), ("TT",)], [("THR",)])
            if t == 1:
                tcopy(T.C16[:], T.M16[:], [("M16",)], [("C16",)])
            elif not last:
                tt(T.C16[:], T.C16[:], T.M16[:], A_.add, [("C16",), ("M16",)], [("C16",)])
        tt(T.E1[:], T.E0[:], T.B16[:], A_.subtract, [("E0",), ("B16",)], [("E1",)])
        kgr = newgroup()
        for n, (l0, l1) in enumerate(CHUNKS):
            s3 = ("S", 16 * l0, 16 * l1)
            r3 = ("RL", 16 * l0, 16 * l1)
            ko = ("KEY", l0, l1)
            a = 4096 + 16 * l0
            for k in range(16):
                tt(T.S[:, l0:l1, k], T.BIG[:, a + k:4096 + 16 * l1:16], T.HP[:, l0:l1], A_.subtract,
                   [("BIG", a, 4096 + 16 * l1), ("HP", 0, 256)], [s3], "s%d_%d" % (t, l0))
            ts(T.RL[:, l0:l1, :], T.S[:, l0:l1, :], -2.0, -2048.0, A_.mult, A_.min, [s3], [r3])
            picks(PICKS[n])
            mm(T.KEY[:, l0:l1], T.IB[:], T.KC[:, l0:l1], True, False, [("IB",), ("KC",)], [ko], kgr)
            for r in range(16):
                mm(T.KEY[:, l0:l1], T.ERM[:, 128 * r:128 * r + 128], T.S[:, l0 + r:l1:16, :], False, False, [("ERM",), s3], [ko], kgr)
            for r in range(16):
                mm(T.KEY[:, l0:l1], T.ERM[:, 128 * r:128 * r + 128], T.RL[:, l0 + r:l1:16, :], False, r == 15, [("ERM",), r3], [ko], kgr)
        picks(PICKS[-1])
        scan(T.PS[:], T.RM[:], T.KEY[:, 0:256], A_.max, A_.min, [("RM",), ("KEY", 0, 256)], [("PS",)])
        mk = T.PS[:, 15:256:16]
        tcopy(T.MKI[:], mk, [("PS",)], [("MKI",)])
        ts(T.MT[:], mk, T.THR[:, 0:1], None, A_.is_lt, None, [("PS",), ("THR",)], [("MT",)])
        ts(T.KWI[:], T.MKI[:], 15, None, A_.bitwise_and, None, [("MKI",)], [("KWI",)])
        tt(T.U1[:], T.KWI[:], T.E1[:], A_.add, [("KWI",), ("E1",)], [("U1",)])
        tt(T.U2[:], T.KWI[:], T.E2[:], A_.add, [("KWI",), ("E2",)], [("U2",)])
        tt(T.U1[:], T.U1[:], T.MT[:], A_.mult, [("U1",), ("MT",)], [("U1",)])
        tt(T.U2[:], T.U2[:], T.MT[:], A_.mult, [("U2",), ("MT",)], [("U2",)])
        tt(T.QF[:], T.U1[:], T.B16[:], A_.add, [("U1",), ("B16",)], [("QF",)])
        tt(T.QXF[:], T.U2[:], T.HI[:], A_.add, [("U2",), ("HI",)], [("QXF",)])
        tcopy(T.QO[:], T.QF[:], [("QF",)], [("QO",)])
        tcopy(T.QXO[:], T.QXF[:], [("QXF",)], [("QXO",)])
        act(T.F1[:], T.BIG[:].indirect(T.QXO[:]), [BW, ("QXO",)], [("F1",)])
        pull(T.BIG[:], BW, "QO")
        weave(place("YO"))
        tt(T.Z[:], T.NX[:].indirect(T.YO[:]), T.DM[:], A_.mult, [("NX",), ("YO",), ("DM",)], [("Z",)])
        ts(T.YL[:], T.FR[:], 8192.0, 2048.0, A_.mult, A_.add, [("FR",)], [("YL",)])
        scan(T.SC[:], T.RS[:], T.Z[:], A_.mult, A_.add, [("RS",), ("Z",)], [("SC",)])
        tcopy(T.VO[:], T.SC[:, 15:256:16], [("SC",)], [("VO",)])
        tcopy(T.VL[:], T.SC[:, 15:256:16], [("SC",)], [("VL",)])
        blend("HA")
        act(T.F1[:], T.BIG[:, 0:4096].indirect(T.VO[:]), [("BIG", 0, 4096), ("VO",)], [("F1",)])
        to_hp("HA")
        pull(T.BIG[:, 0:4096], ("BIG", 0, 4096), "VO")
        tt(T.S2[:], T.F1[:], T.HP[:, 0:256], A_.subtract, [("F1",), ("HP", 0, 256)], [("S2",)])
        ts(T.R2[:], T.S2[:], -2.0, -2048.0, A_.mult, A_.min, [("S2",)], [("R2",)])
        g2 = newgroup()
        for r in range(16):
            mm(T.SM[:, 0:16], T.ERM[:, 128 * r:128 * r + 128], T.S2[:, r:256:16], r == 0, False, [("ERM",), ("S2",)], [("SM", 0, 16)], g2)
        for r in range(16):
            mm(T.SM[:, 0:16], T.ERM[:, 128 * r:128 * r + 128], T.R2[:, r:256:16], False, r == 15, [("ERM",), ("R2",)], [("SM", 0, 16)], g2)
        picks(16)
        weave(place("NL") + [
            lambda: tt(T.W2[:], T.NL[:], T.YL[:], A_.subtract, [("NL",), ("YL",)], [("W2",)]),
            lambda: tt(T.W1[:], T.VL[:], T.HI[:], A_.subtract, [("VL",), ("HI",)], [("W1",)]),
            lambda: tt(T.W2[:], T.W2[:], T.MT[:], A_.mult, [("W2",), ("MT",)], [("W2",)]),
            lambda: tt(T.W1[:], T.W1[:], T.MT[:], A_.mult, [("W1",), ("MT",)], [("W1",)])], codes("YL", "MT", "ABY"))
        gm = newgroup()
        scalar_codes("ABY", range(0, YA))
        if t:
            qg = [] if last else [qfill(i) for i in range(4)]
        ts(T.GO[:], T.SM[:, 0:16], T.TT[:, 1:2], None, A_.is_le, None, [("SM", 0, 16), ("TT",)], [("GO",)])
        tt(T.W2[:], T.W2[:], T.GO[:], A_.mult, [("W2",), ("GO",)], [("W2",)])
        tt(T.W1[:], T.W1[:], T.GO[:], A_.mult, [("W1",), ("GO",)], [("W1",)])
        tt(T.YF[:], T.W2[:], T.YL[:], A_.add, [("W2",), ("YL",)], [("YF",)])
        tt(T.QNF[:], T.W1[:], T.HI[:], A_.add, [("W1",), ("HI",)], [("QNF",)])
        tcopy(T.YFO[:], T.YF[:], [("YF",)], [("YFO",)])
        tcopy(T.QNO[:], T.QNF[:], [("QNF",)], [("QNO",)])
        act(T.F1[:], T.BIG[:].indirect(T.QNO[:]), [BW, ("QNO",)], [("F1",)])
        if not last:
            ks = "KS%d" % t
            tcopy(T[ks][:], T.PL[:].indirect(T.YFO[:]), [("PL",), ("YFO",)], [(ks,)])
            send("K%d" % (t + 1), ks, "rk%d" % t)
        scalar_codes("ABY", range(YA, 16))
        if t == 0:
            setup_last()
        tt(T.U1[:], T.GO[:], T.MT[:], A_.mult, [("GO",), ("MT",)], [("U1",)])
        lj = []
        if t:
            lj = [lambda: tcopy(T.NNI[:], T.CN[:, 256:512], [("CN", 256, 512)], [("NNI",)]), lambda: None,
                  lambda: tt(T.BMF[:], T.CN[:, 256:512], T.NNI[:], A_.subtract, [("CN", 256, 512), ("NNI",)], [("BMF",)])]
        weave(lj, codes("NL", "U1", "ABN"))
        scalar_marks("ABY", range(0, YA), gm)
        if t == 0:
            qg = [qfill(i) for i in range(4)]
            for k in range(16):
                op("A", lambda: S_.activation(T.EX[:, 128 * k:128 * k + 128], T.IF[:], F.Identity, scale=T.OH[:, k:k + 1]), [("IF",), ("OH",)], [("EX", 128 * k, 128 * k + 128)])
        if not last:
            op("V", lambda: V.tensor_reduce(T.CNT[:, 0:1], T.MT[:], AxisListType.X, A_.add), [("MT",)], [("CNT", 0, 1)])
            mm(T.SM[:, 16:17], T.BO[:], T.CNT[:, 0:1], True, True, [("BO",), ("CNT", 0, 1)], [("SM", 16, 17)], newgroup())
        if t == 0:
            tt(T.DX[:], T.KEY[:, 0:256], T.PSG[:], A_.subtract, [("KEY", 0, 256), ("PSG",)], [("DX",)])
        marks("ABN", range(0, 6), gm)
        blend(hs)
        if not last:
            send("H%d" % (t + 1), hs, "rh%d" % t)
        marks("ABN", range(6, 16), gm)
        if t:
            ts(T.JC[:], T.BMF[:], 8192.0, 2048.0, A_.mult, A_.add, [("BMF",)], [("JC",)])
        if not last:
            tcopy(T.PJ[:, 0:1], T.SM[:, 16:17], [("SM", 16, 17)], [("PJ",)])
        scalar_marks("ABY", range(YA, 16), gm)
        tcopy(T.KI[:, 0:128], T.CN[:, 0:128], [("CN", 0, 128)], [("KI", 0, 128)])
        ts(T.M16[:, 128:256], T.CN[:, 0:128], 1023.5, None, A_.is_gt, None, [("CN", 0, 128)], [("M16", 128, 256)])
        ts(T.KI[:, 128:256], T.KI[:, 0:128], 1023, None, A_.bitwise_and, None, [("KI", 0, 128)], [("KI", 128, 256)])
        ts(T.M16[:, 0:128], T.KI[:, 128:256], 0.5, None, A_.is_gt, None, [("KI", 128, 256)], [("M16", 0, 128)])
        tt(T.ZZ[:], T.M16[:], T.DX[:], A_.mult, [("M16",), ("DX",)], [("ZZ",)])
        jold = "JC" if t else "PSG"
        tt(T.JC[:], T[jold][:], T.ZZ[:], A_.add, [(jold,), ("ZZ",)], [("JC",)])
        tcopy(T.LP[:], T.JC[:], [("JC",)], [("LP",)])
        if last:
            halves("JR", "IW", "LP", [("IW",)])
            tcopy(T.YB[:], T.NX[:].indirect(T.YFO[:]), [("NX",), ("YFO",)], [("YB",)])
            ts(T.YH[:], T[hs][:], -1026.0, None, A_.add, None, [(hs,)], [("YH",)])
            dma("S", T.yb[:], T.YB[0:128:16, :], [("YB",)], [])
            dma("S", T.yh[:], T.YH[:], [("YH",)], [])
            halves("Q", "JR", "LP", [("JR",)], 4)
            for j in range(4):
                c = (1024 * j, 1024 * j + 1024)
                dma("S", T.yj[:, c[0]:c[1]], T.Q[0:128:16, c[0]:c[1]], [("Q",) + c], [])
            break
        vb = ["KEY", "HP", "SM"]
        old = "Q" if t else "BIG"
        for i in range(QA // 2):
            if i >= 4:
                qg.append(qfill(i))
            qmark(i, qg[i])
            for a in range(QA + 2 * i, min(QA + 2 * i + 2, 16)):
                r, e = vb[i], a % 2
                w = (r, 256 * e, 256 * e + 256)
                mm(T[r][:, 256 * e:256 * e + 256], T.BR[:, 128 * a:128 * a + 128], T.M16[:], True, True, [("BR",), ("M16",)], [w], newgroup())
        for a in range(QA, 16):
            r, e = vb[(a - QA) // 2 % 3], a % 2
            tt(T.Q[:, a:4096:16], T[r][:, 256 * e:256 * e + 256], T[old][:, a:4096:16], A_.add, [(r, 256 * e, 256 * e + 256), ("Q%d" % a,) if t else ("BIG", 0, 4096)], [("Q%d" % a,)])
        halves("JR", "Q", "LP", [("Q%d" % a,) for a in range(16)])
        halves("BIG", "JR", "LP", [("JR",)])
        arrive("K%d" % (t + 1), "rk%d" % t)
        arrive("H%d" % (t + 1), "rh%d" % t)

    for e in ("V", "A", "T"):
        need("G", "c" + e, count[e])
    need("G", "cG", count["G"])
    for (s, v) in [(k[0], k[1]) for k in snap if k[0][0] == "d"]:
        need("G", s, v)
    for t in range(3):
        need("G", "rk%d" % t, nprv)
        need("G", "rh%d" % t, nprv)
    need("G", "ls", sent[0])
